import numpy as np
import ml_dtypes


def mxq(x, axis, fmt="e4m3"):
    dtype, down = {"e4m3": (ml_dtypes.float8_e4m3fn, 7), "e5m2": (ml_dtypes.float8_e5m2, 14)}[fmt]
    v = np.moveaxis(np.asarray(x, np.float32).astype(ml_dtypes.bfloat16).astype(np.float64), axis, -1)
    blocks = v.reshape(v.shape[:-1] + (-1, 32))
    amax = np.abs(blocks).max(-1, keepdims=True)
    byte = np.maximum(np.where(amax > 0, np.frexp(amax)[1] - 1 + 127, 0) - down, 1)
    scale = np.exp2(byte - 127.0)
    codes = (blocks / scale).astype(np.float32).astype(dtype).astype(np.float64)
    return np.moveaxis((codes * scale).reshape(v.shape), -1, axis)


WIDE = False


def mx_kscale(k):
    if not WIDE:
        return np.ones(k)
    levels = np.array([10, -10, 5, -5, 0])
    if k % 512:
        return np.exp2(np.random.permutation(np.resize(levels, k // 32))).repeat(32)
    a = np.empty((k // 512, 16))
    for p in range(k // 512):
        a[p, :8] = np.random.permutation(np.resize(levels, 8))
        for g in range(8):
            far = levels[np.abs(levels - a[p, g]) >= 10]
            a[p, g + 8] = far[np.random.randint(len(far))]
    return np.exp2(a.ravel()).repeat(32)


def f64(x):
    return np.asarray(x).astype(np.float64)


def striped(idx):
    return np.tile(np.asarray(idx).reshape(-1, 16).T, (8, 1)).astype(np.uint16)


def unstriped(offs):
    return offs[:16].T.reshape(-1).astype(np.int64)


E2M1 = np.array([0.0, 0.5, 1.0, 1.5, 2.0, 3.0, 4.0, 6.0, -0.0, -0.5, -1.0, -1.5, -2.0, -3.0, -4.0, -6.0])


def pack_weight(w, fmt):
    k, n = w.shape
    w = f64(np.asarray(w, np.float32).astype(ml_dtypes.bfloat16)).reshape(k // 32, 32, n)
    amax = np.abs(w).max(1)
    if fmt == "e4m3":
        byte = np.frexp(amax)[1] - 1 + 127 - 7
    else:
        mant, ex = np.frexp(amax / 6.0)
        byte = np.where(mant > 0.5, ex, ex - 1) + 127
    byte = np.clip(np.where(amax > 0, byte, 1), 1, 254)
    scaled = (w * np.exp2(127.0 - byte)[:, None, :]).reshape(k, n).astype(np.float32)
    by_word = np.ascontiguousarray(scaled.reshape(k // 512, 128, 4, n).transpose(0, 1, 3, 2))
    if fmt == "e4m3":
        words = by_word.astype(ml_dtypes.float8_e4m3fn).view(np.uint8)
    else:
        c = by_word.astype(ml_dtypes.float4_e2m1fn).view(np.uint8) & 0xF
        words = (c[..., 0::2] | (c[..., 1::2] << 4)).reshape(k // 512, 128, 2 * n)
    return np.ascontiguousarray(words), np.ascontiguousarray(byte.astype(np.uint8).reshape(k // 512, 16, n))


def unpack_weight(words, scales, fmt):
    g, _, n = scales.shape
    words = np.ascontiguousarray(words).reshape(g, 128, n, -1)
    if fmt == "e4m3":
        vals = words.view(ml_dtypes.float8_e4m3fn).astype(np.float64)
    else:
        nib = np.empty((g, 128, n, 4), np.uint8)
        nib[..., 0::2] = words & 0xF
        nib[..., 1::2] = words >> 4
        vals = E2M1[nib]
    vals = vals * np.repeat(np.exp2(scales.astype(np.float64) - 127.0), 8, axis=1)[..., None]
    return vals.transpose(0, 1, 3, 2).reshape(g * 512, n)


B, N, T, D, NQ = 1, 512, 2048, 512, 256


def setup_inputs():
    n = np.random.standard_normal
    idx = np.random.permutation(T)[:B * N]
    s = mx_kscale(D)[:, None]
    kp = pack_weight(n((D, T)) / s, "e4m3")
    cp = pack_weight(n((D, T)) / s, "e4m3")
    return {
        "qT": (n((B, D, NQ)) * s * (1.00 / np.sqrt(D))).astype(np.float32),
        "k_words": kp[0],
        "k_scales": kp[1],
        "c_words": cp[0],
        "c_scales": cp[1],
        "ls": (np.random.uniform(7.8, 8.4, (B, NQ, 1))).astype(np.float32),
        "l2": (np.random.uniform(7.8, 8.4, (B, NQ, 1))).astype(np.float32),
        "offs": striped(idx),
    }


def reference(qT, k_words, k_scales, c_words, c_scales, ls, l2, offs):
    idx = unstriped(offs)
    pick = lambda x, which: x[:, which].reshape(x.shape[0], B, -1).transpose(1, 0, 2)
    k = unpack_weight(k_words, k_scales, "e4m3")
    kg = pick(k, idx)
    c = unpack_weight(c_words, c_scales, "e4m3")
    cg = pick(c, idx)
    qq = mxq(f64(qT), 1, "e4m3")
    a = qq.transpose(0, 2, 1) @ kg
    z = qq.transpose(0, 2, 1) @ cg
    y = np.maximum(np.exp(a - f64(ls)) - np.exp(z - f64(l2)), 0.0)
    return y

@@ -1,0 +1,134 @@
+from contextlib import ExitStack
+
+import concourse.mybir as mybir
+
+N, T, D, NQ = 512, 2048, 512, 256
+FLOPS = 2 * 2 * NQ * D * N
+
+F32 = mybir.dt.float32
+BF16 = mybir.dt.bfloat16
+I32 = mybir.dt.int32
+U32 = mybir.dt.uint32
+U16 = mybir.dt.uint16
+U8 = mybir.dt.uint8
+FP8X4 = mybir.dt.float8_e4m3fn_x4
+ACT = mybir.ActivationFunctionType
+
+P = 128
+PACK = 4
+QT = NQ // P
+HALF = N // 2
+K_ROW, C_ROW = 0, 4
+L2_COL = 8
+
+
+def tile_attend_dupkl_topk_kernel(tc, qT, k_words, k_scales, c_words, c_scales, ls, l2, offs, out):
+    nc = tc.nc
+    with ExitStack() as ctx:
+        keep = ctx.enter_context(tc.tile_pool(name="keep", bufs=1))
+        psum = ctx.enter_context(tc.psum_pool(name="psum", bufs=1))
+
+        offsets = keep.tile([P, N // 16], U16, name="offsets")
+        q_raw = keep.tile([P, PACK, NQ], F32, name="q_raw", align_bytes=64)
+        k_pool = keep.tile([P, T], I32, name="k_pool", align_bytes=64)
+        c_pool = keep.tile([P, T], I32, name="c_pool", align_bytes=64)
+        ks_pool = keep.tile([P, T // 4], I32, name="ks_pool", align_bytes=64)
+        cs_pool = keep.tile([P, T // 4], I32, name="cs_pool", align_bytes=64)
+        lse = keep.tile([P, 2 * L2_COL], F32, name="lse", align_bytes=64)
+        warm = keep.tile([P, 8], F32, name="warm", align_bytes=64)
+        warm_out = keep.tile([P, 8], F32, name="warm_out", align_bytes=64)
+
+        nc.sync.dma_start(offsets[:], offs)
+        nc.sync.dma_start(q_raw[:], qT[0].rearrange("(p j) w -> p j w", j=PACK))
+        nc.sync.dma_start(k_pool[:], k_words[0].rearrange("p n t -> p (n t)").bitcast(I32))
+        nc.sync.dma_start(c_pool[:], c_words[0].rearrange("p n t -> p (n t)").bitcast(I32))
+
+        nc.vector.memset(cs_pool[:], 0)
+        nc.vector.memset(ks_pool[:], 0)
+        nc.vector.memset(lse[:], 0.0)
+        nc.vector.memset(warm[:], 0.0)
+
+        def load_scale_rows(engine, pool_tile, scales, row0, j):
+            rows = scales[0].bitcast(I32).rearrange("(q j) n -> j q n", j=4)
+            engine.dma_start(pool_tile[row0 + j : P : 32, :], rows[j])
+
+        for j in range(4):
+            load_scale_rows(nc.scalar, ks_pool, k_scales, K_ROW, j)
+        nc.scalar.activation(warm_out[:], warm[:], ACT.Exp)
+        for j in range(4):
+            load_scale_rows(nc.scalar if j < 2 else nc.gpsimd, cs_pool, c_scales, C_ROW, j)
+        nc.gpsimd.dma_start(lse[:, 0:QT], ls[0].rearrange("(p t) o -> p (t o)", t=QT))
+        nc.gpsimd.dma_start(lse[:, L2_COL : L2_COL + QT], l2[0].rearrange("(p t) o -> p (t o)", t=QT))
+
+        ks = keep.tile([P, N], U8, name="ks", align_bytes=64)
+        nc.vector.tensor_copy(ks[:], ks_pool[:].bitcast(U8).indirect(offsets[:]))
+
+        q_bf = keep.tile([P, QT, P, PACK], BF16, name="q_bf", align_bytes=64)
+        nc.scalar.copy(q_bf[:], q_raw[:].rearrange("p j (m t) -> p t m j", t=QT))
+        q_codes = keep.tile([P, NQ], U32, name="q_codes", align_bytes=64)
+        q_scales = keep.tile([P, NQ], U8, name="q_scales", align_bytes=64)
+        nc.vector.quantize_mx(
+            out=q_codes[:].bitcast(FP8X4),
+            scales=q_scales[:],
+            in_=q_bf[:].rearrange("p t m j -> p (t m j)"),
+        )
+
+        cs = keep.tile([P, N], U8, name="cs", align_bytes=64)
+        nc.vector.tensor_copy(cs[:], cs_pool[:].bitcast(U8).indirect(offsets[:]))
+        kw = keep.tile([P, N], U32, name="kw", align_bytes=64)
+        nc.vector.tensor_copy(kw[:], k_pool[:].bitcast(U32).indirect(offsets[:]))
+
+        neg = keep.tile([P, 2 * L2_COL], F32, name="neg", align_bytes=64)
+        nc.scalar.mul(neg[:], lse[:], -1.0)
+
+        ea = keep.tile([P, QT, N], F32, name="ea", align_bytes=64)
+        for t in range(QT):
+            a = psum.tile([P, N], F32, name=f"a{t}")
+            nc.tensor.matmul_mx(
+                out=a[:],
+                lhsT=q_codes[:, t * P : (t + 1) * P].bitcast(FP8X4),
+                lhsT_scale=q_scales[:, t * P : (t + 1) * P],
+                rhs=kw[:].bitcast(FP8X4),
+                rhs_scale=ks[K_ROW:P, :],
+                start=True,
+                stop=True,
+            )
+            nc.scalar.activation(ea[:, t, :], a[:], ACT.Exp, bias=neg[:, t : t + 1])
+
+        cw = []
+        for h in range(2):
+            cw_h = keep.tile([P, HALF], U32, name=f"cw{h}", align_bytes=64)
+            nc.vector.tensor_copy(
+                cw_h[:], c_pool[:].bitcast(U32).indirect(offsets[:, h * HALF // 16 : (h + 1) * HALF // 16])
+            )
+            cw.append(cw_h)
+
+        ez = {}
+        for h in range(2):
+            for t in range(QT):
+                z = psum.tile([P, HALF], F32, name=f"z{h}{t}")
+                nc.tensor.matmul_mx(
+                    out=z[:],
+                    lhsT=q_codes[:, t * P : (t + 1) * P].bitcast(FP8X4),
+                    lhsT_scale=q_scales[:, t * P : (t + 1) * P],
+                    rhs=cw[h][:].bitcast(FP8X4),
+                    rhs_scale=cs[C_ROW:P, h * HALF : (h + 1) * HALF],
+                    start=True,
+                    stop=True,
+                )
+                ez[h, t] = keep.tile([P, HALF], F32, name=f"ez{h}{t}", align_bytes=64)
+                nc.scalar.activation(ez[h, t][:], z[:], ACT.Exp, bias=neg[:, L2_COL + t : L2_COL + t + 1])
+
+        out_v = out[0].rearrange("(p t) n -> p t n", t=QT)
+        diff = keep.tile([P, 2, QT, HALF], F32, name="diff", align_bytes=64)
+        res = keep.tile([P, 2, QT, HALF], F32, name="res", align_bytes=64)
+        for t in range(QT):
+            nc.vector.tensor_sub(diff[:, 0, t, :], ea[:, t, 0:HALF], ez[0, t][:])
+        nc.vector.tensor_sub(diff[:, 1, 0, :], ea[:, 0, HALF:N], ez[1, 0][:])
+        nc.vector.tensor_scalar_max(res[:, 0, :, :], diff[:, 0, :, :], 0.0)
+        nc.sync.dma_start(out_v[:, :, 0:HALF], res[:, 0, :, :])
+        nc.vector.tensor_sub(diff[:, 1, 1, :], ea[:, 1, HALF:N], ez[1, 1][:])
+        nc.scalar.activation(res[:, 1, 0, :], diff[:, 1, 0, :], ACT.Relu)
+        nc.sync.dma_start(out_v[:, 0, HALF:N], res[:, 1, 0, :])
+        nc.vector.tensor_scalar_max(res[:, 1, 1, :], diff[:, 1, 1, :], 0.0)
+        nc.sync.dma_start(out_v[:, 1, HALF:N], res[:, 1, 1, :])

@@ -34,31 +34,34 @@ def tile_attend_dupkl_topk_kernel(tc, qT, k_words, k_scales, c_words, c_scales, 
         c_pool = keep.tile([P, T], I32, name="c_pool", align_bytes=64)
         ks_pool = keep.tile([P, T // 4], I32, name="ks_pool", align_bytes=64)
         cs_pool = keep.tile([P, T // 4], I32, name="cs_pool", align_bytes=64)
-        lse = keep.tile([P, 2 * L2_COL], F32, name="lse", align_bytes=64)
+        ls_sb = keep.tile([P, QT], F32, name="ls_sb", align_bytes=64)
+        l2_sb = keep.tile([P, QT], F32, name="l2_sb", align_bytes=64)
         warm = keep.tile([P, 8], F32, name="warm", align_bytes=64)
         warm_out = keep.tile([P, 8], F32, name="warm_out", align_bytes=64)
 
+        nc.vector.memset(ks_pool[:, 0:320], 0)
+        nc.gpsimd.memset(ks_pool[:, 320:512], 0)
+        nc.vector.memset(warm[:], 0.0)
+        nc.vector.memset(cs_pool[:], 0)
+        nc.scalar.activation(warm_out[:], warm[:], ACT.Exp)
+
+        def load_scale_rows(pool_tile, scales, row0):
+            rows = scales[0].bitcast(I32).rearrange("(q j) n -> j q n", j=4)
+            for j in range(4):
+                nc.sync.dma_start(pool_tile[row0 + j : P : 32, :], rows[j])
+
         nc.sync.dma_start(offsets[:], offs)
         nc.sync.dma_start(q_raw[:], qT[0].rearrange("(p j) w -> p j w", j=PACK))
+        nc.sync.dma_start(ls_sb[:], ls[0].rearrange("(p t) o -> p (t o)", t=QT))
+        nc.sync.dma_start(l2_sb[:], l2[0].rearrange("(p t) o -> p (t o)", t=QT))
+        load_scale_rows(ks_pool, k_scales, K_ROW)
         nc.sync.dma_start(k_pool[:], k_words[0].rearrange("p n t -> p (n t)").bitcast(I32))
+        load_scale_rows(cs_pool, c_scales, C_ROW)
         nc.sync.dma_start(c_pool[:], c_words[0].rearrange("p n t -> p (n t)").bitcast(I32))
 
-        nc.vector.memset(cs_pool[:], 0)
-        nc.vector.memset(ks_pool[:], 0)
-        nc.vector.memset(lse[:], 0.0)
-        nc.vector.memset(warm[:], 0.0)
-
-        def load_scale_rows(engine, pool_tile, scales, row0, j):
-            rows = scales[0].bitcast(I32).rearrange("(q j) n -> j q n", j=4)
-            engine.dma_start(pool_tile[row0 + j : P : 32, :], rows[j])
-
-        for j in range(4):
-            load_scale_rows(nc.scalar, ks_pool, k_scales, K_ROW, j)
-        nc.scalar.activation(warm_out[:], warm[:], ACT.Exp)
-        for j in range(4):
-            load_scale_rows(nc.scalar if j < 2 else nc.gpsimd, cs_pool, c_scales, C_ROW, j)
-        nc.gpsimd.dma_start(lse[:, 0:QT], ls[0].rearrange("(p t) o -> p (t o)", t=QT))
-        nc.gpsimd.dma_start(lse[:, L2_COL : L2_COL + QT], l2[0].rearrange("(p t) o -> p (t o)", t=QT))
+        neg = keep.tile([P, 2 * L2_COL], F32, name="neg", align_bytes=64)
+        nc.scalar.mul(neg[:, 0:QT], ls_sb[:], -1.0)
+        nc.scalar.mul(neg[:, L2_COL : L2_COL + QT], l2_sb[:], -1.0)
 
         ks = keep.tile([P, N], U8, name="ks", align_bytes=64)
         nc.vector.tensor_copy(ks[:], ks_pool[:].bitcast(U8).indirect(offsets[:]))
@@ -73,13 +76,10 @@ def tile_attend_dupkl_topk_kernel(tc, qT, k_words, k_scales, c_words, c_scales, 
             in_=q_bf[:].rearrange("p t m j -> p (t m j)"),
         )
 
-        cs = keep.tile([P, N], U8, name="cs", align_bytes=64)
-        nc.vector.tensor_copy(cs[:], cs_pool[:].bitcast(U8).indirect(offsets[:]))
         kw = keep.tile([P, N], U32, name="kw", align_bytes=64)
         nc.vector.tensor_copy(kw[:], k_pool[:].bitcast(U32).indirect(offsets[:]))
-
-        neg = keep.tile([P, 2 * L2_COL], F32, name="neg", align_bytes=64)
-        nc.scalar.mul(neg[:], lse[:], -1.0)
+        cs = keep.tile([P, N], U8, name="cs", align_bytes=64)
+        nc.vector.tensor_copy(cs[:], cs_pool[:].bitcast(U8).indirect(offsets[:]))
 
         ea = keep.tile([P, QT, N], F32, name="ea", align_bytes=64)
         for t in range(QT):

@@ -20,6 +20,7 @@ QT = NQ // P
 HALF = N // 2
 K_ROW, C_ROW = 0, 4
 L2_COL = 8
+K_HEAD = 256
 
 
 def tile_attend_dupkl_topk_kernel(tc, qT, k_words, k_scales, c_words, c_scales, ls, l2, offs, out):
@@ -39,8 +40,7 @@ def tile_attend_dupkl_topk_kernel(tc, qT, k_words, k_scales, c_words, c_scales, 
         warm = keep.tile([P, 8], F32, name="warm", align_bytes=64)
         warm_out = keep.tile([P, 8], F32, name="warm_out", align_bytes=64)
 
-        nc.vector.memset(ks_pool[:, 0:320], 0)
-        nc.gpsimd.memset(ks_pool[:, 320:512], 0)
+        nc.vector.memset(ks_pool[:], 0)
         nc.vector.memset(warm[:], 0.0)
         nc.vector.memset(cs_pool[:], 0)
         nc.scalar.activation(warm_out[:], warm[:], ACT.Exp)
@@ -53,15 +53,16 @@ def tile_attend_dupkl_topk_kernel(tc, qT, k_words, k_scales, c_words, c_scales, 
         nc.sync.dma_start(offsets[:], offs)
         nc.sync.dma_start(q_raw[:], qT[0].rearrange("(p j) w -> p j w", j=PACK))
         nc.sync.dma_start(ls_sb[:], ls[0].rearrange("(p t) o -> p (t o)", t=QT))
-        nc.sync.dma_start(l2_sb[:], l2[0].rearrange("(p t) o -> p (t o)", t=QT))
+        k_rows = k_words[0].rearrange("p n t -> p (n t)").bitcast(I32)
+        nc.sync.dma_start(k_pool[:, 0:K_HEAD], k_rows[:, 0:K_HEAD])
         load_scale_rows(ks_pool, k_scales, K_ROW)
-        nc.sync.dma_start(k_pool[:], k_words[0].rearrange("p n t -> p (n t)").bitcast(I32))
+        nc.sync.dma_start(k_pool[:, K_HEAD:T], k_rows[:, K_HEAD:T])
         load_scale_rows(cs_pool, c_scales, C_ROW)
         nc.sync.dma_start(c_pool[:], c_words[0].rearrange("p n t -> p (n t)").bitcast(I32))
+        nc.sync.dma_start(l2_sb[:], l2[0].rearrange("(p t) o -> p (t o)", t=QT))
 
         neg = keep.tile([P, 2 * L2_COL], F32, name="neg", align_bytes=64)
         nc.scalar.mul(neg[:, 0:QT], ls_sb[:], -1.0)
-        nc.scalar.mul(neg[:, L2_COL : L2_COL + QT], l2_sb[:], -1.0)
 
         ks = keep.tile([P, N], U8, name="ks", align_bytes=64)
         nc.vector.tensor_copy(ks[:], ks_pool[:].bitcast(U8).indirect(offsets[:]))
@@ -95,6 +96,8 @@ def tile_attend_dupkl_topk_kernel(tc, qT, k_words, k_scales, c_words, c_scales, 
             )
             nc.scalar.activation(ea[:, t, :], a[:], ACT.Exp, bias=neg[:, t : t + 1])
 
+        nc.scalar.mul(neg[:, L2_COL : L2_COL + QT], l2_sb[:], -1.0)
+
         cw = []
         for h in range(2):
             cw_h = keep.tile([P, HALF], U32, name=f"cw{h}", align_bytes=64)
@@ -103,32 +106,52 @@ def tile_attend_dupkl_topk_kernel(tc, qT, k_words, k_scales, c_words, c_scales, 
             )
             cw.append(cw_h)
 
-        ez = {}
-        for h in range(2):
-            for t in range(QT):
-                z = psum.tile([P, HALF], F32, name=f"z{h}{t}")
-                nc.tensor.matmul_mx(
-                    out=z[:],
-                    lhsT=q_codes[:, t * P : (t + 1) * P].bitcast(FP8X4),
-                    lhsT_scale=q_scales[:, t * P : (t + 1) * P],
-                    rhs=cw[h][:].bitcast(FP8X4),
-                    rhs_scale=cs[C_ROW:P, h * HALF : (h + 1) * HALF],
-                    start=True,
-                    stop=True,
-                )
-                ez[h, t] = keep.tile([P, HALF], F32, name=f"ez{h}{t}", align_bytes=64)
-                nc.scalar.activation(ez[h, t][:], z[:], ACT.Exp, bias=neg[:, L2_COL + t : L2_COL + t + 1])
+        pieces = [(0, 0, 128), (0, 128, 128), (1, 0, 256), (0, 256, 256), (1, 256, 128), (1, 384, 128)]
+        ez = []
+        for i, (t, n0, width) in enumerate(pieces):
+            h = n0 // HALF
+            z = psum.tile([P, width], F32, name=f"z{i}")
+            nc.tensor.matmul_mx(
+                out=z[:],
+                lhsT=q_codes[:, t * P : (t + 1) * P].bitcast(FP8X4),
+                lhsT_scale=q_scales[:, t * P : (t + 1) * P],
+                rhs=cw[h][:, n0 - h * HALF : n0 - h * HALF + width].bitcast(FP8X4),
+                rhs_scale=cs[C_ROW:P, n0 : n0 + width],
+                start=True,
+                stop=True,
+            )
+            ez_i = keep.tile([P, width], F32, name=f"ez{i}", align_bytes=64)
+            nc.scalar.activation(ez_i[:], z[:], ACT.Exp, bias=neg[:, L2_COL + t : L2_COL + t + 1])
+            ez.append(ez_i)
 
         out_v = out[0].rearrange("(p t) n -> p t n", t=QT)
-        diff = keep.tile([P, 2, QT, HALF], F32, name="diff", align_bytes=64)
-        res = keep.tile([P, 2, QT, HALF], F32, name="res", align_bytes=64)
-        for t in range(QT):
-            nc.vector.tensor_sub(diff[:, 0, t, :], ea[:, t, 0:HALF], ez[0, t][:])
-        nc.vector.tensor_sub(diff[:, 1, 0, :], ea[:, 0, HALF:N], ez[1, 0][:])
-        nc.vector.tensor_scalar_max(res[:, 0, :, :], diff[:, 0, :, :], 0.0)
-        nc.sync.dma_start(out_v[:, :, 0:HALF], res[:, 0, :, :])
-        nc.vector.tensor_sub(diff[:, 1, 1, :], ea[:, 1, HALF:N], ez[1, 1][:])
-        nc.scalar.activation(res[:, 1, 0, :], diff[:, 1, 0, :], ACT.Relu)
-        nc.sync.dma_start(out_v[:, 0, HALF:N], res[:, 1, 0, :])
-        nc.vector.tensor_scalar_max(res[:, 1, 1, :], diff[:, 1, 1, :], 0.0)
-        nc.sync.dma_start(out_v[:, 1, HALF:N], res[:, 1, 1, :])
+        diff = keep.tile([P, QT, N], F32, name="diff", align_bytes=64)
+        res = keep.tile([P, QT, N], F32, name="res", align_bytes=64)
+
+        def sub(i):
+            t, n0, width = pieces[i]
+            nc.vector.tensor_sub(diff[:, t, n0 : n0 + width], ea[:, t, n0 : n0 + width], ez[i][:])
+
+        def clamp_v(t, n0, n1):
+            nc.vector.tensor_scalar_max(res[:, t, n0:n1], diff[:, t, n0:n1], 0.0)
+
+        def clamp_s(t, n0, n1):
+            nc.scalar.activation(res[:, t, n0:n1], diff[:, t, n0:n1], ACT.Relu)
+
+        def store(t, n0, n1):
+            nc.sync.dma_start(out_v[:, t, n0:n1], res[:, t, n0:n1])
+
+        sub(0)
+        sub(1)
+        clamp_v(0, 0, 256)
+        store(0, 0, 256)
+        sub(2)
+        sub(3)
+        sub(4)
+        sub(5)
+        clamp_s(1, 0, 256)
+        store(1, 0, 256)
+        clamp_s(0, 256, 512)
+        store(0, 256, 512)
+        clamp_v(1, 256, 512)
+        store(1, 256, 512)

@@ -18,9 +18,10 @@ P = 128
 PACK = 4
 QT = NQ // P
 HALF = N // 2
-K_ROW, C_ROW = 0, 4
+SPREAD = 8
+C_FIRST = 80
 L2_COL = 8
-K_HEAD = 256
+W = 128
 
 
 def tile_attend_dupkl_topk_kernel(tc, qT, k_words, k_scales, c_words, c_scales, ls, l2, offs, out):
@@ -30,11 +31,11 @@ def tile_attend_dupkl_topk_kernel(tc, qT, k_words, k_scales, c_words, c_scales, 
         psum = ctx.enter_context(tc.psum_pool(name="psum", bufs=1))
 
         offsets = keep.tile([P, N // 16], U16, name="offsets")
-        q_raw = keep.tile([P, PACK, NQ], F32, name="q_raw", align_bytes=64)
+        q_raw = keep.tile([P, PACK, NQ], F32, name="q_raw", tag="q_then_planes", align_bytes=64)
         k_pool = keep.tile([P, T], I32, name="k_pool", align_bytes=64)
         c_pool = keep.tile([P, T], I32, name="c_pool", align_bytes=64)
         ks_pool = keep.tile([P, T // 4], I32, name="ks_pool", align_bytes=64)
-        cs_pool = keep.tile([P, T // 4], I32, name="cs_pool", align_bytes=64)
+        cs_pool = keep.tile([P, T // 4], I32, name="cs_pool", tag="ks_then_q", align_bytes=64)
         ls_sb = keep.tile([P, QT], F32, name="ls_sb", align_bytes=64)
         l2_sb = keep.tile([P, QT], F32, name="l2_sb", align_bytes=64)
         warm = keep.tile([P, 8], F32, name="warm", align_bytes=64)
@@ -42,34 +43,44 @@ def tile_attend_dupkl_topk_kernel(tc, qT, k_words, k_scales, c_words, c_scales, 
 
         nc.vector.memset(ks_pool[:], 0)
         nc.vector.memset(warm[:], 0.0)
-        nc.vector.memset(cs_pool[:], 0)
+        for p0, p1 in ((0, 64), (64, C_FIRST), (C_FIRST + 16, P)):
+            nc.vector.memset(cs_pool[p0:p1, :], 0)
         nc.scalar.activation(warm_out[:], warm[:], ACT.Exp)
 
-        def load_scale_rows(pool_tile, scales, row0):
-            rows = scales[0].bitcast(I32).rearrange("(q j) n -> j q n", j=4)
-            for j in range(4):
-                nc.sync.dma_start(pool_tile[row0 + j : P : 32, :], rows[j])
-
         nc.sync.dma_start(offsets[:], offs)
-        nc.sync.dma_start(q_raw[:], qT[0].rearrange("(p j) w -> p j w", j=PACK))
+        nc.sync.dma_start(cs_pool[C_FIRST : C_FIRST + 16, :], c_scales[0].bitcast(I32))
         nc.sync.dma_start(ls_sb[:], ls[0].rearrange("(p t) o -> p (t o)", t=QT))
-        k_rows = k_words[0].rearrange("p n t -> p (n t)").bitcast(I32)
-        nc.sync.dma_start(k_pool[:, 0:K_HEAD], k_rows[:, 0:K_HEAD])
-        load_scale_rows(ks_pool, k_scales, K_ROW)
-        nc.sync.dma_start(k_pool[:, K_HEAD:T], k_rows[:, K_HEAD:T])
-        load_scale_rows(cs_pool, c_scales, C_ROW)
-        nc.sync.dma_start(c_pool[:], c_words[0].rearrange("p n t -> p (n t)").bitcast(I32))
         nc.sync.dma_start(l2_sb[:], l2[0].rearrange("(p t) o -> p (t o)", t=QT))
+        nc.sync.dma_start(ks_pool[0:P:SPREAD, :], k_scales[0].bitcast(I32))
+        nc.sync.dma_start(q_raw[:], qT[0].rearrange("(p j) w -> p j w", j=PACK))
+        nc.sync.dma_start(k_pool[:], k_words[0].rearrange("p n t -> p (n t)").bitcast(I32))
+        nc.sync.dma_start(c_pool[:], c_words[0].rearrange("p n t -> p (n t)").bitcast(I32))
 
         neg = keep.tile([P, 2 * L2_COL], F32, name="neg", align_bytes=64)
         nc.scalar.mul(neg[:, 0:QT], ls_sb[:], -1.0)
+        nc.scalar.mul(neg[:, L2_COL : L2_COL + QT], l2_sb[:], -1.0)
 
-        ks = keep.tile([P, N], U8, name="ks", align_bytes=64)
-        nc.vector.tensor_copy(ks[:], ks_pool[:].bitcast(U8).indirect(offsets[:]))
+        ks_rows = keep.tile([P, N], U8, name="ks_rows", align_bytes=64)
+        nc.vector.tensor_copy(ks_rows[:], ks_pool[:].bitcast(U8).indirect(offsets[:]))
+        cs_rows = keep.tile([P, N], U8, name="cs_rows", align_bytes=64)
+        nc.vector.tensor_copy(cs_rows[:], cs_pool[:].bitcast(U8).indirect(offsets[:]))
 
         q_bf = keep.tile([P, QT, P, PACK], BF16, name="q_bf", align_bytes=64)
         nc.scalar.copy(q_bf[:], q_raw[:].rearrange("p j (m t) -> p t m j", t=QT))
-        q_codes = keep.tile([P, NQ], U32, name="q_codes", align_bytes=64)
+        planes = keep.tile([P, 2 * N // 4], I32, name="planes", tag="q_then_planes", align_bytes=64)
+        k_plane = planes[:, 0 : N // 4]
+        c_plane = planes[:, N // 4 : 2 * N // 4]
+        nc.vector.tensor_copy(k_plane, ks_rows[:].bitcast(I32))
+        nc.vector.memset(c_plane, 0)
+        for j in range(1, 4):
+            nc.scalar.dma_start(planes[j:P:32, 0 : N // 4], ks_rows[SPREAD * j : P : 32, :].bitcast(I32))
+        for j in range(4):
+            nc.scalar.dma_start(
+                planes[j:P:32, N // 4 : 2 * N // 4], cs_rows[C_FIRST + j : C_FIRST + 16 : 4, :].bitcast(I32)
+            )
+        ks = k_plane.bitcast(U8)
+        cs = c_plane.bitcast(U8)
+        q_codes = keep.tile([P, NQ], U32, name="q_codes", tag="ks_then_q", align_bytes=64)
         q_scales = keep.tile([P, NQ], U8, name="q_scales", align_bytes=64)
         nc.vector.quantize_mx(
             out=q_codes[:].bitcast(FP8X4),
@@ -79,8 +90,6 @@ def tile_attend_dupkl_topk_kernel(tc, qT, k_words, k_scales, c_words, c_scales, 
 
         kw = keep.tile([P, N], U32, name="kw", align_bytes=64)
         nc.vector.tensor_copy(kw[:], k_pool[:].bitcast(U32).indirect(offsets[:]))
-        cs = keep.tile([P, N], U8, name="cs", align_bytes=64)
-        nc.vector.tensor_copy(cs[:], cs_pool[:].bitcast(U8).indirect(offsets[:]))
 
         ea = keep.tile([P, QT, N], F32, name="ea", align_bytes=64)
         for t in range(QT):
@@ -90,13 +99,11 @@ def tile_attend_dupkl_topk_kernel(tc, qT, k_words, k_scales, c_words, c_scales, 
                 lhsT=q_codes[:, t * P : (t + 1) * P].bitcast(FP8X4),
                 lhsT_scale=q_scales[:, t * P : (t + 1) * P],
                 rhs=kw[:].bitcast(FP8X4),
-                rhs_scale=ks[K_ROW:P, :],
+                rhs_scale=ks,
                 start=True,
                 stop=True,
             )
             nc.scalar.activation(ea[:, t, :], a[:], ACT.Exp, bias=neg[:, t : t + 1])
-
-        nc.scalar.mul(neg[:, L2_COL : L2_COL + QT], l2_sb[:], -1.0)
 
         cw = []
         for h in range(2):
@@ -106,9 +113,10 @@ def tile_attend_dupkl_topk_kernel(tc, qT, k_words, k_scales, c_words, c_scales, 
             )
             cw.append(cw_h)
 
-        pieces = [(0, 0, 128), (0, 128, 128), (1, 0, 256), (0, 256, 256), (1, 256, 128), (1, 384, 128)]
+        products = [(0, 0, 128), (0, 128, 128), (1, 0, 256), (0, 256, 256), (1, 256, 256)]
+        pieces = []
         ez = []
-        for i, (t, n0, width) in enumerate(pieces):
+        for i, (t, n0, width) in enumerate(products):
             h = n0 // HALF
             z = psum.tile([P, width], F32, name=f"z{i}")
             nc.tensor.matmul_mx(
@@ -116,21 +124,24 @@ def tile_attend_dupkl_topk_kernel(tc, qT, k_words, k_scales, c_words, c_scales, 
                 lhsT=q_codes[:, t * P : (t + 1) * P].bitcast(FP8X4),
                 lhsT_scale=q_scales[:, t * P : (t + 1) * P],
                 rhs=cw[h][:, n0 - h * HALF : n0 - h * HALF + width].bitcast(FP8X4),
-                rhs_scale=cs[C_ROW:P, n0 : n0 + width],
+                rhs_scale=cs[:, n0 : n0 + width],
                 start=True,
                 stop=True,
             )
-            ez_i = keep.tile([P, width], F32, name=f"ez{i}", align_bytes=64)
-            nc.scalar.activation(ez_i[:], z[:], ACT.Exp, bias=neg[:, L2_COL + t : L2_COL + t + 1])
-            ez.append(ez_i)
+            for w0 in range(0, width, W):
+                w = min(W, width)
+                ez_i = keep.tile([P, w], F32, name=f"ez{len(ez)}", align_bytes=64)
+                nc.scalar.activation(ez_i[:], z[:, w0 : w0 + w], ACT.Exp, bias=neg[:, L2_COL + t : L2_COL + t + 1])
+                ez.append(ez_i)
+                pieces.append((t, n0 + w0, w))
 
         out_v = out[0].rearrange("(p t) n -> p t n", t=QT)
         diff = keep.tile([P, QT, N], F32, name="diff", align_bytes=64)
         res = keep.tile([P, QT, N], F32, name="res", align_bytes=64)
 
         def sub(i):
-            t, n0, width = pieces[i]
-            nc.vector.tensor_sub(diff[:, t, n0 : n0 + width], ea[:, t, n0 : n0 + width], ez[i][:])
+            t, n0, w = pieces[i]
+            nc.vector.tensor_sub(diff[:, t, n0 : n0 + w], ea[:, t, n0 : n0 + w], ez[i][:])
 
         def clamp_v(t, n0, n1):
             nc.vector.tensor_scalar_max(res[:, t, n0:n1], diff[:, t, n0:n1], 0.0)
@@ -143,15 +154,17 @@ def tile_attend_dupkl_topk_kernel(tc, qT, k_words, k_scales, c_words, c_scales, 
 
         sub(0)
         sub(1)
+        sub(2)
         clamp_v(0, 0, 256)
         store(0, 0, 256)
-        sub(2)
         sub(3)
         sub(4)
         sub(5)
+        sub(6)
+        sub(7)
         clamp_s(1, 0, 256)
         store(1, 0, 256)
-        clamp_s(0, 256, 512)
+        clamp_v(0, 256, 512)
         store(0, 256, 512)
         clamp_v(1, 256, 512)
         store(1, 256, 512)

@@ -18,8 +18,10 @@ P = 128
 PACK = 4
 QT = NQ // P
 HALF = N // 2
-SPREAD = 8
-C_FIRST = 80
+ROWS = 16
+K_FIRST = 112
+C_FIRST = 48
+C_HEAD = 512
 L2_COL = 8
 W = 128
 
@@ -31,30 +33,36 @@ def tile_attend_dupkl_topk_kernel(tc, qT, k_words, k_scales, c_words, c_scales, 
         psum = ctx.enter_context(tc.psum_pool(name="psum", bufs=1))
 
         offsets = keep.tile([P, N // 16], U16, name="offsets")
-        q_raw = keep.tile([P, PACK, NQ], F32, name="q_raw", tag="q_then_planes", align_bytes=64)
+        q_raw = keep.tile([P, PACK, NQ], F32, name="q_raw", align_bytes=64)
         k_pool = keep.tile([P, T], I32, name="k_pool", align_bytes=64)
-        c_pool = keep.tile([P, T], I32, name="c_pool", align_bytes=64)
-        ks_pool = keep.tile([P, T // 4], I32, name="ks_pool", align_bytes=64)
-        cs_pool = keep.tile([P, T // 4], I32, name="cs_pool", tag="ks_then_q", align_bytes=64)
+        c_head = keep.tile([P, C_HEAD], I32, name="c_head", align_bytes=64)
+        ks_pool = keep.tile([P, T // 4], I32, name="ks_pool", tag="ks_then_c", align_bytes=64)
+        cs_pool = keep.tile([P, T // 4], I32, name="cs_pool", tag="cs_then_q", align_bytes=64)
         ls_sb = keep.tile([P, QT], F32, name="ls_sb", align_bytes=64)
         l2_sb = keep.tile([P, QT], F32, name="l2_sb", align_bytes=64)
         warm = keep.tile([P, 8], F32, name="warm", align_bytes=64)
         warm_out = keep.tile([P, 8], F32, name="warm_out", align_bytes=64)
 
-        nc.vector.memset(ks_pool[:], 0)
+        k_plane = keep.tile([P, N // 4], I32, name="k_plane", align_bytes=64)
+        c_plane = keep.tile([P, N // 4], I32, name="c_plane", align_bytes=64)
+
+        nc.vector.memset(ks_pool[0:K_FIRST, :], 0)
         nc.vector.memset(warm[:], 0.0)
-        for p0, p1 in ((0, 64), (64, C_FIRST), (C_FIRST + 16, P)):
-            nc.vector.memset(cs_pool[p0:p1, :], 0)
+        nc.vector.memset(cs_pool[0:C_FIRST, :], 0)
+        nc.vector.memset(cs_pool[C_FIRST + ROWS : P, :], 0)
+        nc.vector.memset(k_plane[:], 0)
+        nc.vector.memset(c_plane[:], 0)
         nc.scalar.activation(warm_out[:], warm[:], ACT.Exp)
 
         nc.sync.dma_start(offsets[:], offs)
-        nc.sync.dma_start(cs_pool[C_FIRST : C_FIRST + 16, :], c_scales[0].bitcast(I32))
+        nc.sync.dma_start(ks_pool[K_FIRST : K_FIRST + ROWS, :], k_scales[0].bitcast(I32))
+        nc.sync.dma_start(cs_pool[C_FIRST : C_FIRST + ROWS, :], c_scales[0].bitcast(I32))
         nc.sync.dma_start(ls_sb[:], ls[0].rearrange("(p t) o -> p (t o)", t=QT))
         nc.sync.dma_start(l2_sb[:], l2[0].rearrange("(p t) o -> p (t o)", t=QT))
-        nc.sync.dma_start(ks_pool[0:P:SPREAD, :], k_scales[0].bitcast(I32))
         nc.sync.dma_start(q_raw[:], qT[0].rearrange("(p j) w -> p j w", j=PACK))
         nc.sync.dma_start(k_pool[:], k_words[0].rearrange("p n t -> p (n t)").bitcast(I32))
-        nc.sync.dma_start(c_pool[:], c_words[0].rearrange("p n t -> p (n t)").bitcast(I32))
+        c_rows = c_words[0].rearrange("p n t -> p (n t)").bitcast(I32)
+        nc.sync.dma_start(c_head[:], c_rows[:, 0:C_HEAD])
 
         neg = keep.tile([P, 2 * L2_COL], F32, name="neg", align_bytes=64)
         nc.scalar.mul(neg[:, 0:QT], ls_sb[:], -1.0)
@@ -62,25 +70,23 @@ def tile_attend_dupkl_topk_kernel(tc, qT, k_words, k_scales, c_words, c_scales, 
 
         ks_rows = keep.tile([P, N], U8, name="ks_rows", align_bytes=64)
         nc.vector.tensor_copy(ks_rows[:], ks_pool[:].bitcast(U8).indirect(offsets[:]))
+        for j in range(4):
+            queue = nc.sync if j < 2 else nc.scalar
+            queue.dma_start(k_plane[j:P:32, :], ks_rows[K_FIRST + j : K_FIRST + ROWS : 4, :].bitcast(I32))
+        c_pool = keep.tile([P, T], I32, name="c_pool", tag="ks_then_c", align_bytes=64)
+        nc.sync.dma_start(c_pool[:, C_HEAD:T], c_rows[:, C_HEAD:T])
         cs_rows = keep.tile([P, N], U8, name="cs_rows", align_bytes=64)
         nc.vector.tensor_copy(cs_rows[:], cs_pool[:].bitcast(U8).indirect(offsets[:]))
 
         q_bf = keep.tile([P, QT, P, PACK], BF16, name="q_bf", align_bytes=64)
         nc.scalar.copy(q_bf[:], q_raw[:].rearrange("p j (m t) -> p t m j", t=QT))
-        planes = keep.tile([P, 2 * N // 4], I32, name="planes", tag="q_then_planes", align_bytes=64)
-        k_plane = planes[:, 0 : N // 4]
-        c_plane = planes[:, N // 4 : 2 * N // 4]
-        nc.vector.tensor_copy(k_plane, ks_rows[:].bitcast(I32))
-        nc.vector.memset(c_plane, 0)
-        for j in range(1, 4):
-            nc.scalar.dma_start(planes[j:P:32, 0 : N // 4], ks_rows[SPREAD * j : P : 32, :].bitcast(I32))
         for j in range(4):
-            nc.scalar.dma_start(
-                planes[j:P:32, N // 4 : 2 * N // 4], cs_rows[C_FIRST + j : C_FIRST + 16 : 4, :].bitcast(I32)
+            nc.sync.dma_start(
+                c_plane[j:P:32, :], cs_rows[C_FIRST + j : C_FIRST + ROWS : 4, :].bitcast(I32)
             )
-        ks = k_plane.bitcast(U8)
-        cs = c_plane.bitcast(U8)
-        q_codes = keep.tile([P, NQ], U32, name="q_codes", tag="ks_then_q", align_bytes=64)
+        ks = k_plane[:].bitcast(U8)
+        cs = c_plane[:].bitcast(U8)
+        q_codes = keep.tile([P, NQ], U32, name="q_codes", tag="cs_then_q", align_bytes=64)
         q_scales = keep.tile([P, NQ], U8, name="q_scales", align_bytes=64)
         nc.vector.quantize_mx(
             out=q_codes[:].bitcast(FP8X4),
@@ -90,6 +96,7 @@ def tile_attend_dupkl_topk_kernel(tc, qT, k_words, k_scales, c_words, c_scales, 
 
         kw = keep.tile([P, N], U32, name="kw", align_bytes=64)
         nc.vector.tensor_copy(kw[:], k_pool[:].bitcast(U32).indirect(offsets[:]))
+        nc.vector.tensor_copy(c_pool[:, 0:C_HEAD], c_head[:])
 
         ea = keep.tile([P, QT, N], F32, name="ea", align_bytes=64)
         for t in range(QT):

@@ -21,7 +21,7 @@ HALF = N // 2
 ROWS = 16
 K_FIRST = 112
 C_FIRST = 48
-C_HEAD = 512
+C_HEAD = 384
 L2_COL = 8
 W = 128
 
@@ -55,10 +55,10 @@ def tile_attend_dupkl_topk_kernel(tc, qT, k_words, k_scales, c_words, c_scales, 
         nc.scalar.activation(warm_out[:], warm[:], ACT.Exp)
 
         nc.sync.dma_start(offsets[:], offs)
-        nc.sync.dma_start(ks_pool[K_FIRST : K_FIRST + ROWS, :], k_scales[0].bitcast(I32))
-        nc.sync.dma_start(cs_pool[C_FIRST : C_FIRST + ROWS, :], c_scales[0].bitcast(I32))
-        nc.sync.dma_start(ls_sb[:], ls[0].rearrange("(p t) o -> p (t o)", t=QT))
-        nc.sync.dma_start(l2_sb[:], l2[0].rearrange("(p t) o -> p (t o)", t=QT))
+        nc.scalar.dma_start(ks_pool[K_FIRST : K_FIRST + ROWS, :], k_scales[0].bitcast(I32))
+        nc.scalar.dma_start(cs_pool[C_FIRST : C_FIRST + ROWS, :], c_scales[0].bitcast(I32))
+        nc.scalar.dma_start(ls_sb[:], ls[0].rearrange("(p t) o -> p (t o)", t=QT))
+        nc.scalar.dma_start(l2_sb[:], l2[0].rearrange("(p t) o -> p (t o)", t=QT))
         nc.sync.dma_start(q_raw[:], qT[0].rearrange("(p j) w -> p j w", j=PACK))
         nc.sync.dma_start(k_pool[:], k_words[0].rearrange("p n t -> p (n t)").bitcast(I32))
         c_rows = c_words[0].rearrange("p n t -> p (n t)").bitcast(I32)
@@ -71,8 +71,7 @@ def tile_attend_dupkl_topk_kernel(tc, qT, k_words, k_scales, c_words, c_scales, 
         ks_rows = keep.tile([P, N], U8, name="ks_rows", align_bytes=64)
         nc.vector.tensor_copy(ks_rows[:], ks_pool[:].bitcast(U8).indirect(offsets[:]))
         for j in range(4):
-            queue = nc.sync if j < 2 else nc.scalar
-            queue.dma_start(k_plane[j:P:32, :], ks_rows[K_FIRST + j : K_FIRST + ROWS : 4, :].bitcast(I32))
+            nc.sync.dma_start(k_plane[j:P:32, :], ks_rows[K_FIRST + j : K_FIRST + ROWS : 4, :].bitcast(I32))
         c_pool = keep.tile([P, T], I32, name="c_pool", tag="ks_then_c", align_bytes=64)
         nc.sync.dma_start(c_pool[:, C_HEAD:T], c_rows[:, C_HEAD:T])
         cs_rows = keep.tile([P, N], U8, name="cs_rows", align_bytes=64)

@@ -56,10 +56,10 @@ def tile_attend_dupkl_topk_kernel(tc, qT, k_words, k_scales, c_words, c_scales, 
 
         nc.sync.dma_start(offsets[:], offs)
         nc.scalar.dma_start(ks_pool[K_FIRST : K_FIRST + ROWS, :], k_scales[0].bitcast(I32))
-        nc.scalar.dma_start(cs_pool[C_FIRST : C_FIRST + ROWS, :], c_scales[0].bitcast(I32))
-        nc.scalar.dma_start(ls_sb[:], ls[0].rearrange("(p t) o -> p (t o)", t=QT))
-        nc.scalar.dma_start(l2_sb[:], l2[0].rearrange("(p t) o -> p (t o)", t=QT))
         nc.sync.dma_start(q_raw[:], qT[0].rearrange("(p j) w -> p j w", j=PACK))
+        nc.sync.dma_start(cs_pool[C_FIRST : C_FIRST + ROWS, :], c_scales[0].bitcast(I32))
+        nc.sync.dma_start(ls_sb[:], ls[0].rearrange("(p t) o -> p (t o)", t=QT))
+        nc.sync.dma_start(l2_sb[:], l2[0].rearrange("(p t) o -> p (t o)", t=QT))
         nc.sync.dma_start(k_pool[:], k_words[0].rearrange("p n t -> p (n t)").bitcast(I32))
         c_rows = c_words[0].rearrange("p n t -> p (n t)").bitcast(I32)
         nc.sync.dma_start(c_head[:], c_rows[:, 0:C_HEAD])
@@ -93,23 +93,30 @@ def tile_attend_dupkl_topk_kernel(tc, qT, k_words, k_scales, c_words, c_scales, 
             in_=q_bf[:].rearrange("p t m j -> p (t m j)"),
         )
 
-        kw = keep.tile([P, N], U32, name="kw", align_bytes=64)
-        nc.vector.tensor_copy(kw[:], k_pool[:].bitcast(U32).indirect(offsets[:]))
+        kw = []
+        for h in range(2):
+            kw_h = keep.tile([P, HALF], U32, name=f"kw{h}", align_bytes=64)
+            nc.vector.tensor_copy(
+                kw_h[:], k_pool[:].bitcast(U32).indirect(offsets[:, h * HALF // 16 : (h + 1) * HALF // 16])
+            )
+            kw.append(kw_h)
         nc.vector.tensor_copy(c_pool[:, 0:C_HEAD], c_head[:])
 
         ea = keep.tile([P, QT, N], F32, name="ea", align_bytes=64)
+        a = [psum.tile([P, N], F32, name=f"a{t}") for t in range(QT)]
+        for h in range(2):
+            for t in range(QT):
+                nc.tensor.matmul_mx(
+                    out=a[t][:, h * HALF : (h + 1) * HALF],
+                    lhsT=q_codes[:, t * P : (t + 1) * P].bitcast(FP8X4),
+                    lhsT_scale=q_scales[:, t * P : (t + 1) * P],
+                    rhs=kw[h][:].bitcast(FP8X4),
+                    rhs_scale=ks[:, h * HALF : (h + 1) * HALF],
+                    start=True,
+                    stop=True,
+                )
         for t in range(QT):
-            a = psum.tile([P, N], F32, name=f"a{t}")
-            nc.tensor.matmul_mx(
-                out=a[:],
-                lhsT=q_codes[:, t * P : (t + 1) * P].bitcast(FP8X4),
-                lhsT_scale=q_scales[:, t * P : (t + 1) * P],
-                rhs=kw[:].bitcast(FP8X4),
-                rhs_scale=ks,
-                start=True,
-                stop=True,
-            )
-            nc.scalar.activation(ea[:, t, :], a[:], ACT.Exp, bias=neg[:, t : t + 1])
+            nc.scalar.activation(ea[:, t, :], a[t][:], ACT.Exp, bias=neg[:, t : t + 1])
 
         cw = []
         for h in range(2):

@@ -1,6 +1,7 @@
 from contextlib import ExitStack
 
 import concourse.mybir as mybir
+from concourse.masks import make_identity
 
 N, T, D, NQ = 512, 2048, 512, 256
 FLOPS = 2 * 2 * NQ * D * N
@@ -21,8 +22,8 @@ HALF = N // 2
 ROWS = 16
 K_FIRST = 112
 C_FIRST = 48
-C_HEAD = 384
-L2_COL = 8
+C_HEAD = 512
+LSE_ROW = P - 2
 W = 128
 
 
@@ -38,8 +39,8 @@ def tile_attend_dupkl_topk_kernel(tc, qT, k_words, k_scales, c_words, c_scales, 
         c_head = keep.tile([P, C_HEAD], I32, name="c_head", align_bytes=64)
         ks_pool = keep.tile([P, T // 4], I32, name="ks_pool", tag="ks_then_c", align_bytes=64)
         cs_pool = keep.tile([P, T // 4], I32, name="cs_pool", tag="cs_then_q", align_bytes=64)
-        ls_sb = keep.tile([P, QT], F32, name="ls_sb", align_bytes=64)
-        l2_sb = keep.tile([P, QT], F32, name="l2_sb", align_bytes=64)
+        lse_rows = keep.tile([P, NQ], F32, name="lse_rows", align_bytes=64)
+        ident = keep.tile([P, P], F32, name="ident", align_bytes=64)
         warm = keep.tile([P, 8], F32, name="warm", align_bytes=64)
         warm_out = keep.tile([P, 8], F32, name="warm_out", align_bytes=64)
 
@@ -52,21 +53,25 @@ def tile_attend_dupkl_topk_kernel(tc, qT, k_words, k_scales, c_words, c_scales, 
         nc.vector.memset(cs_pool[C_FIRST + ROWS : P, :], 0)
         nc.vector.memset(k_plane[:], 0)
         nc.vector.memset(c_plane[:], 0)
+        nc.gpsimd.memset(lse_rows[0:LSE_ROW, :], 0.0)
+        make_identity(nc, ident[:])
         nc.scalar.activation(warm_out[:], warm[:], ACT.Exp)
 
         nc.sync.dma_start(offsets[:], offs)
         nc.scalar.dma_start(ks_pool[K_FIRST : K_FIRST + ROWS, :], k_scales[0].bitcast(I32))
         nc.sync.dma_start(q_raw[:], qT[0].rearrange("(p j) w -> p j w", j=PACK))
         nc.sync.dma_start(cs_pool[C_FIRST : C_FIRST + ROWS, :], c_scales[0].bitcast(I32))
-        nc.sync.dma_start(ls_sb[:], ls[0].rearrange("(p t) o -> p (t o)", t=QT))
-        nc.sync.dma_start(l2_sb[:], l2[0].rearrange("(p t) o -> p (t o)", t=QT))
+        nc.sync.dma_start(lse_rows[LSE_ROW : LSE_ROW + 1, :], ls[0].rearrange("q o -> o q"))
+        nc.sync.dma_start(lse_rows[LSE_ROW + 1 : P, :], l2[0].rearrange("q o -> o q"))
         nc.sync.dma_start(k_pool[:], k_words[0].rearrange("p n t -> p (n t)").bitcast(I32))
         c_rows = c_words[0].rearrange("p n t -> p (n t)").bitcast(I32)
         nc.sync.dma_start(c_head[:], c_rows[:, 0:C_HEAD])
 
-        neg = keep.tile([P, 2 * L2_COL], F32, name="neg", align_bytes=64)
-        nc.scalar.mul(neg[:, 0:QT], ls_sb[:], -1.0)
-        nc.scalar.mul(neg[:, L2_COL : L2_COL + QT], l2_sb[:], -1.0)
+        lse_cols = psum.tile([P, QT, P], F32, name="lse_cols")
+        for t in range(QT):
+            nc.tensor.transpose(lse_cols[:, t, :], lse_rows[:, t:NQ:QT], ident[:])
+        neg = keep.tile([P, QT, 2], F32, name="neg", align_bytes=64)
+        nc.scalar.mul(neg[:], lse_cols[:, :, LSE_ROW:P], -1.0)
 
         ks_rows = keep.tile([P, N], U8, name="ks_rows", align_bytes=64)
         nc.vector.tensor_copy(ks_rows[:], ks_pool[:].bitcast(U8).indirect(offsets[:]))
@@ -116,7 +121,7 @@ def tile_attend_dupkl_topk_kernel(tc, qT, k_words, k_scales, c_words, c_scales, 
                     stop=True,
                 )
         for t in range(QT):
-            nc.scalar.activation(ea[:, t, :], a[t][:], ACT.Exp, bias=neg[:, t : t + 1])
+            nc.scalar.activation(ea[:, t, :], a[t][:], ACT.Exp, bias=neg[:, t, 0:1])
 
         cw = []
         for h in range(2):
@@ -144,7 +149,7 @@ def tile_attend_dupkl_topk_kernel(tc, qT, k_words, k_scales, c_words, c_scales, 
             for w0 in range(0, width, W):
                 w = min(W, width)
                 ez_i = keep.tile([P, w], F32, name=f"ez{len(ez)}", align_bytes=64)
-                nc.scalar.activation(ez_i[:], z[:, w0 : w0 + w], ACT.Exp, bias=neg[:, L2_COL + t : L2_COL + t + 1])
+                nc.scalar.activation(ez_i[:], z[:, w0 : w0 + w], ACT.Exp, bias=neg[:, t, 1:2])
                 ez.append(ez_i)
                 pieces.append((t, n0 + w0, w))
 

@@ -67,7 +67,7 @@ def tile_attend_dupkl_topk_kernel(tc, qT, k_words, k_scales, c_words, c_scales, 
         c_rows = c_words[0].rearrange("p n t -> p (n t)").bitcast(I32)
         nc.sync.dma_start(c_head[:], c_rows[:, 0:C_HEAD])
 
-        lse_cols = psum.tile([P, QT, P], F32, name="lse_cols")
+        lse_cols = psum.tile([P, QT, P], F32, name="lse_cols", tag="spare_bank")
         for t in range(QT):
             nc.tensor.transpose(lse_cols[:, t, :], lse_rows[:, t:NQ:QT], ident[:])
         neg = keep.tile([P, QT, 2], F32, name="neg", align_bytes=64)
@@ -120,6 +120,17 @@ def tile_attend_dupkl_topk_kernel(tc, qT, k_words, k_scales, c_words, c_scales, 
                     start=True,
                     stop=True,
                 )
+        spare = psum.tile([P, QT, HALF], F32, name="spare", tag="spare_bank")
+        for t in range(QT):
+            nc.tensor.matmul_mx(
+                out=spare[:, t, :],
+                lhsT=q_codes[:, t * P : (t + 1) * P].bitcast(FP8X4),
+                lhsT_scale=q_scales[:, t * P : (t + 1) * P],
+                rhs=kw[1][:].bitcast(FP8X4),
+                rhs_scale=ks[:, HALF:N],
+                start=True,
+                stop=True,
+            )
         for t in range(QT):
             nc.scalar.activation(ea[:, t, :], a[t][:], ACT.Exp, bias=neg[:, t, 0:1])
 

@@ -98,6 +98,18 @@ def tile_attend_dupkl_topk_kernel(tc, qT, k_words, k_scales, c_words, c_scales, 
             in_=q_bf[:].rearrange("p t m j -> p (t m j)"),
         )
 
+        spare = psum.tile([P, QT, HALF], F32, name="spare", tag="spare_bank")
+        for t in range(QT):
+            nc.tensor.matmul_mx(
+                out=spare[:, t, :],
+                lhsT=q_codes[:, t * P : (t + 1) * P].bitcast(FP8X4),
+                lhsT_scale=q_scales[:, t * P : (t + 1) * P],
+                rhs=q_codes[:].bitcast(FP8X4),
+                rhs_scale=q_scales[:],
+                start=True,
+                stop=True,
+            )
+
         kw = []
         for h in range(2):
             kw_h = keep.tile([P, HALF], U32, name=f"kw{h}", align_bytes=64)
@@ -108,11 +120,11 @@ def tile_attend_dupkl_topk_kernel(tc, qT, k_words, k_scales, c_words, c_scales, 
         nc.vector.tensor_copy(c_pool[:, 0:C_HEAD], c_head[:])
 
         ea = keep.tile([P, QT, N], F32, name="ea", align_bytes=64)
-        a = [psum.tile([P, N], F32, name=f"a{t}") for t in range(QT)]
+        a = [psum.tile([P, QT, HALF], F32, name=f"a{h}") for h in range(2)]
         for h in range(2):
             for t in range(QT):
                 nc.tensor.matmul_mx(
-                    out=a[t][:, h * HALF : (h + 1) * HALF],
+                    out=a[h][:, t, :],
                     lhsT=q_codes[:, t * P : (t + 1) * P].bitcast(FP8X4),
                     lhsT_scale=q_scales[:, t * P : (t + 1) * P],
                     rhs=kw[h][:].bitcast(FP8X4),
@@ -120,19 +132,11 @@ def tile_attend_dupkl_topk_kernel(tc, qT, k_words, k_scales, c_words, c_scales, 
                     start=True,
                     stop=True,
                 )
-        spare = psum.tile([P, QT, HALF], F32, name="spare", tag="spare_bank")
-        for t in range(QT):
-            nc.tensor.matmul_mx(
-                out=spare[:, t, :],
-                lhsT=q_codes[:, t * P : (t + 1) * P].bitcast(FP8X4),
-                lhsT_scale=q_scales[:, t * P : (t + 1) * P],
-                rhs=kw[1][:].bitcast(FP8X4),
-                rhs_scale=ks[:, HALF:N],
-                start=True,
-                stop=True,
-            )
-        for t in range(QT):
-            nc.scalar.activation(ea[:, t, :], a[t][:], ACT.Exp, bias=neg[:, t, 0:1])
+        for h in range(2):
+            for t in range(QT):
+                nc.scalar.activation(
+                    ea[:, t, h * HALF : (h + 1) * HALF], a[h][:, t, :], ACT.Exp, bias=neg[:, t, 0:1]
+                )
 
         cw = []
         for h in range(2):

@@ -22,7 +22,7 @@ HALF = N // 2
 ROWS = 16
 K_FIRST = 112
 C_FIRST = 48
-C_HEAD = 512
+C_HEAD = 768
 LSE_ROW = P - 2
 W = 128
 

@@ -69,7 +69,7 @@ def tile_attend_dupkl_topk_kernel(tc, qT, k_words, k_scales, c_words, c_scales, 
 
         lse_cols = psum.tile([P, QT, P], F32, name="lse_cols", tag="spare_bank")
         for t in range(QT):
-            nc.tensor.transpose(lse_cols[:, t, :], lse_rows[:, t:NQ:QT], ident[:])
+            nc.tensor.transpose(lse_cols[:, t, :], lse_rows[:, t * P : (t + 1) * P], ident[:])
         neg = keep.tile([P, QT, 2], F32, name="neg", align_bytes=64)
         nc.scalar.mul(neg[:], lse_cols[:, :, LSE_ROW:P], -1.0)
 
@@ -83,7 +83,7 @@ def tile_attend_dupkl_topk_kernel(tc, qT, k_words, k_scales, c_words, c_scales, 
         nc.vector.tensor_copy(cs_rows[:], cs_pool[:].bitcast(U8).indirect(offsets[:]))
 
         q_bf = keep.tile([P, QT, P, PACK], BF16, name="q_bf", align_bytes=64)
-        nc.scalar.copy(q_bf[:], q_raw[:].rearrange("p j (m t) -> p t m j", t=QT))
+        nc.scalar.copy(q_bf[:], q_raw[:].rearrange("p j (t m) -> p t m j", t=QT))
         for j in range(4):
             nc.sync.dma_start(
                 c_plane[j:P:32, :], cs_rows[C_FIRST + j : C_FIRST + ROWS : 4, :].bitcast(I32)
@@ -168,7 +168,7 @@ def tile_attend_dupkl_topk_kernel(tc, qT, k_words, k_scales, c_words, c_scales, 
                 ez.append(ez_i)
                 pieces.append((t, n0 + w0, w))
 
-        out_v = out[0].rearrange("(p t) n -> p t n", t=QT)
+        out_v = out[0].rearrange("(t p) n -> p t n", t=QT)
         diff = keep.tile([P, QT, N], F32, name="diff", align_bytes=64)
         res = keep.tile([P, QT, N], F32, name="res", align_bytes=64)
 
@@ -188,9 +188,9 @@ def tile_attend_dupkl_topk_kernel(tc, qT, k_words, k_scales, c_words, c_scales, 
         sub(0)
         sub(1)
         sub(2)
+        sub(3)
         clamp_v(0, 0, 256)
         store(0, 0, 256)
-        sub(3)
         sub(4)
         sub(5)
         sub(6)

@@ -19,12 +19,14 @@ P = 128
 PACK = 4
 QT = NQ // P
 HALF = N // 2
+PER_COLUMN = 16
 ROWS = 16
+QUADRANT = 32
 K_FIRST = 112
 C_FIRST = 48
-C_HEAD = 768
 LSE_ROW = P - 2
-W = 128
+C_HEAD = 768
+PIECE = 128
 
 
 def tile_attend_dupkl_topk_kernel(tc, qT, k_words, k_scales, c_words, c_scales, ls, l2, offs, out):
@@ -33,29 +35,24 @@ def tile_attend_dupkl_topk_kernel(tc, qT, k_words, k_scales, c_words, c_scales, 
         keep = ctx.enter_context(tc.tile_pool(name="keep", bufs=1))
         psum = ctx.enter_context(tc.psum_pool(name="psum", bufs=1))
 
-        offsets = keep.tile([P, N // 16], U16, name="offsets")
+        offsets = keep.tile([P, N // PER_COLUMN], U16, name="offsets")
         q_raw = keep.tile([P, PACK, NQ], F32, name="q_raw", align_bytes=64)
         k_pool = keep.tile([P, T], I32, name="k_pool", align_bytes=64)
         c_head = keep.tile([P, C_HEAD], I32, name="c_head", align_bytes=64)
-        ks_pool = keep.tile([P, T // 4], I32, name="ks_pool", tag="ks_then_c", align_bytes=64)
-        cs_pool = keep.tile([P, T // 4], I32, name="cs_pool", tag="cs_then_q", align_bytes=64)
+        ks_pool = keep.tile([P, T // PACK], I32, name="ks_pool", tag="ks_then_c", align_bytes=64)
+        cs_pool = keep.tile([P, T // PACK], I32, name="cs_pool", tag="cs_then_q", align_bytes=64)
         lse_rows = keep.tile([P, NQ], F32, name="lse_rows", align_bytes=64)
         ident = keep.tile([P, P], F32, name="ident", align_bytes=64)
-        warm = keep.tile([P, 8], F32, name="warm", align_bytes=64)
-        warm_out = keep.tile([P, 8], F32, name="warm_out", align_bytes=64)
-
-        k_plane = keep.tile([P, N // 4], I32, name="k_plane", align_bytes=64)
-        c_plane = keep.tile([P, N // 4], I32, name="c_plane", align_bytes=64)
+        k_plane = keep.tile([P, N // PACK], I32, name="k_plane", align_bytes=64)
+        c_plane = keep.tile([P, N // PACK], I32, name="c_plane", align_bytes=64)
 
         nc.vector.memset(ks_pool[0:K_FIRST, :], 0)
-        nc.vector.memset(warm[:], 0.0)
         nc.vector.memset(cs_pool[0:C_FIRST, :], 0)
         nc.vector.memset(cs_pool[C_FIRST + ROWS : P, :], 0)
         nc.vector.memset(k_plane[:], 0)
         nc.vector.memset(c_plane[:], 0)
         nc.gpsimd.memset(lse_rows[0:LSE_ROW, :], 0.0)
         make_identity(nc, ident[:])
-        nc.scalar.activation(warm_out[:], warm[:], ACT.Exp)
 
         nc.sync.dma_start(offsets[:], offs)
         nc.scalar.dma_start(ks_pool[K_FIRST : K_FIRST + ROWS, :], k_scales[0].bitcast(I32))
@@ -67,16 +64,19 @@ def tile_attend_dupkl_topk_kernel(tc, qT, k_words, k_scales, c_words, c_scales, 
         c_rows = c_words[0].rearrange("p n t -> p (n t)").bitcast(I32)
         nc.sync.dma_start(c_head[:], c_rows[:, 0:C_HEAD])
 
-        lse_cols = psum.tile([P, QT, P], F32, name="lse_cols", tag="spare_bank")
+        lse_cols = psum.tile([P, QT, P], F32, name="lse_cols")
         for t in range(QT):
             nc.tensor.transpose(lse_cols[:, t, :], lse_rows[:, t * P : (t + 1) * P], ident[:])
         neg = keep.tile([P, QT, 2], F32, name="neg", align_bytes=64)
         nc.scalar.mul(neg[:], lse_cols[:, :, LSE_ROW:P], -1.0)
 
+        def move_to_plane(plane, rows, first):
+            for j in range(PACK):
+                nc.sync.dma_start(plane[j:P:QUADRANT, :], rows[first + j : first + ROWS : PACK, :].bitcast(I32))
+
         ks_rows = keep.tile([P, N], U8, name="ks_rows", align_bytes=64)
         nc.vector.tensor_copy(ks_rows[:], ks_pool[:].bitcast(U8).indirect(offsets[:]))
-        for j in range(4):
-            nc.sync.dma_start(k_plane[j:P:32, :], ks_rows[K_FIRST + j : K_FIRST + ROWS : 4, :].bitcast(I32))
+        move_to_plane(k_plane, ks_rows, K_FIRST)
         c_pool = keep.tile([P, T], I32, name="c_pool", tag="ks_then_c", align_bytes=64)
         nc.sync.dma_start(c_pool[:, C_HEAD:T], c_rows[:, C_HEAD:T])
         cs_rows = keep.tile([P, N], U8, name="cs_rows", align_bytes=64)
@@ -84,12 +84,9 @@ def tile_attend_dupkl_topk_kernel(tc, qT, k_words, k_scales, c_words, c_scales, 
 
         q_bf = keep.tile([P, QT, P, PACK], BF16, name="q_bf", align_bytes=64)
         nc.scalar.copy(q_bf[:], q_raw[:].rearrange("p j (t m) -> p t m j", t=QT))
-        for j in range(4):
-            nc.sync.dma_start(
-                c_plane[j:P:32, :], cs_rows[C_FIRST + j : C_FIRST + ROWS : 4, :].bitcast(I32)
-            )
-        ks = k_plane[:].bitcast(U8)
-        cs = c_plane[:].bitcast(U8)
+        move_to_plane(c_plane, cs_rows, C_FIRST)
+        k_bytes = k_plane[:].bitcast(U8)
+        c_bytes = c_plane[:].bitcast(U8)
         q_codes = keep.tile([P, NQ], U32, name="q_codes", tag="cs_then_q", align_bytes=64)
         q_scales = keep.tile([P, NQ], U8, name="q_scales", align_bytes=64)
         nc.vector.quantize_mx(
@@ -98,106 +95,76 @@ def tile_attend_dupkl_topk_kernel(tc, qT, k_words, k_scales, c_words, c_scales, 
             in_=q_bf[:].rearrange("p t m j -> p (t m j)"),
         )
 
-        spare = psum.tile([P, QT, HALF], F32, name="spare", tag="spare_bank")
-        for t in range(QT):
+        def gather_words(pool, name):
+            halves = []
+            for h in range(2):
+                words = keep.tile([P, HALF], U32, name=f"{name}{h}", align_bytes=64)
+                entries = offsets[:, h * HALF // PER_COLUMN : (h + 1) * HALF // PER_COLUMN]
+                nc.vector.tensor_copy(words[:], pool[:].bitcast(U32).indirect(entries))
+                halves.append(words)
+            return halves
+
+        def product(scores, t, halves, scale_bytes, n0, width):
+            h, at = divmod(n0, HALF)
             nc.tensor.matmul_mx(
-                out=spare[:, t, :],
+                out=scores,
                 lhsT=q_codes[:, t * P : (t + 1) * P].bitcast(FP8X4),
                 lhsT_scale=q_scales[:, t * P : (t + 1) * P],
-                rhs=q_codes[:].bitcast(FP8X4),
-                rhs_scale=q_scales[:],
+                rhs=halves[h][:, at : at + width].bitcast(FP8X4),
+                rhs_scale=scale_bytes[:, n0 : n0 + width],
                 start=True,
                 stop=True,
             )
 
-        kw = []
-        for h in range(2):
-            kw_h = keep.tile([P, HALF], U32, name=f"kw{h}", align_bytes=64)
-            nc.vector.tensor_copy(
-                kw_h[:], k_pool[:].bitcast(U32).indirect(offsets[:, h * HALF // 16 : (h + 1) * HALF // 16])
-            )
-            kw.append(kw_h)
+        kw = gather_words(k_pool, "kw")
         nc.vector.tensor_copy(c_pool[:, 0:C_HEAD], c_head[:])
-
         ea = keep.tile([P, QT, N], F32, name="ea", align_bytes=64)
         a = [psum.tile([P, QT, HALF], F32, name=f"a{h}") for h in range(2)]
         for h in range(2):
             for t in range(QT):
-                nc.tensor.matmul_mx(
-                    out=a[h][:, t, :],
-                    lhsT=q_codes[:, t * P : (t + 1) * P].bitcast(FP8X4),
-                    lhsT_scale=q_scales[:, t * P : (t + 1) * P],
-                    rhs=kw[h][:].bitcast(FP8X4),
-                    rhs_scale=ks[:, h * HALF : (h + 1) * HALF],
-                    start=True,
-                    stop=True,
-                )
+                product(a[h][:, t, :], t, kw, k_bytes, h * HALF, HALF)
         for h in range(2):
             for t in range(QT):
                 nc.scalar.activation(
                     ea[:, t, h * HALF : (h + 1) * HALF], a[h][:, t, :], ACT.Exp, bias=neg[:, t, 0:1]
                 )
 
-        cw = []
-        for h in range(2):
-            cw_h = keep.tile([P, HALF], U32, name=f"cw{h}", align_bytes=64)
-            nc.vector.tensor_copy(
-                cw_h[:], c_pool[:].bitcast(U32).indirect(offsets[:, h * HALF // 16 : (h + 1) * HALF // 16])
-            )
-            cw.append(cw_h)
+        cw = gather_words(c_pool, "cw")
+        blocks = [(h, t) for h in range(2) for t in range(QT)]
+        ez = {}
+        for b, (h, t) in enumerate(blocks):
+            width = PIECE if b == 0 else HALF
+            for n0 in range(h * HALF, (h + 1) * HALF, width):
+                z = psum.tile([P, width], F32, name=f"z{t}_{n0}")
+                product(z[:], t, cw, c_bytes, n0, width)
+                for at in range(0, width, PIECE):
+                    piece = keep.tile([P, PIECE], F32, name=f"ez{t}_{n0 + at}", align_bytes=64)
+                    nc.scalar.activation(piece[:], z[:, at : at + PIECE], ACT.Exp, bias=neg[:, t, 1:2])
+                    ez[(t, n0 + at)] = piece
 
-        products = [(0, 0, 128), (0, 128, 128), (1, 0, 256), (0, 256, 256), (1, 256, 256)]
-        pieces = []
-        ez = []
-        for i, (t, n0, width) in enumerate(products):
-            h = n0 // HALF
-            z = psum.tile([P, width], F32, name=f"z{i}")
-            nc.tensor.matmul_mx(
-                out=z[:],
-                lhsT=q_codes[:, t * P : (t + 1) * P].bitcast(FP8X4),
-                lhsT_scale=q_scales[:, t * P : (t + 1) * P],
-                rhs=cw[h][:, n0 - h * HALF : n0 - h * HALF + width].bitcast(FP8X4),
-                rhs_scale=cs[:, n0 : n0 + width],
-                start=True,
-                stop=True,
-            )
-            for w0 in range(0, width, W):
-                w = min(W, width)
-                ez_i = keep.tile([P, w], F32, name=f"ez{len(ez)}", align_bytes=64)
-                nc.scalar.activation(ez_i[:], z[:, w0 : w0 + w], ACT.Exp, bias=neg[:, t, 1:2])
-                ez.append(ez_i)
-                pieces.append((t, n0 + w0, w))
-
-        out_v = out[0].rearrange("(t p) n -> p t n", t=QT)
+        out_tiles = out[0].rearrange("(t p) n -> p t n", t=QT)
         diff = keep.tile([P, QT, N], F32, name="diff", align_bytes=64)
         res = keep.tile([P, QT, N], F32, name="res", align_bytes=64)
 
-        def sub(i):
-            t, n0, w = pieces[i]
-            nc.vector.tensor_sub(diff[:, t, n0 : n0 + w], ea[:, t, n0 : n0 + w], ez[i][:])
+        def subtract(block):
+            h, t = block
+            for n0 in range(h * HALF, (h + 1) * HALF, PIECE):
+                nc.vector.tensor_sub(diff[:, t, n0 : n0 + PIECE], ea[:, t, n0 : n0 + PIECE], ez[(t, n0)][:])
 
-        def clamp_v(t, n0, n1):
-            nc.vector.tensor_scalar_max(res[:, t, n0:n1], diff[:, t, n0:n1], 0.0)
+        def clamp_and_store(block, on_scalar):
+            h, t = block
+            cols = slice(h * HALF, (h + 1) * HALF)
+            if on_scalar:
+                nc.scalar.activation(res[:, t, cols], diff[:, t, cols], ACT.Relu)
+            else:
+                nc.vector.tensor_scalar_max(res[:, t, cols], diff[:, t, cols], 0.0)
+            nc.sync.dma_start(out_tiles[:, t, cols], res[:, t, cols])
 
-        def clamp_s(t, n0, n1):
-            nc.scalar.activation(res[:, t, n0:n1], diff[:, t, n0:n1], ACT.Relu)
-
-        def store(t, n0, n1):
-            nc.sync.dma_start(out_v[:, t, n0:n1], res[:, t, n0:n1])
-
-        sub(0)
-        sub(1)
-        sub(2)
-        sub(3)
-        clamp_v(0, 0, 256)
-        store(0, 0, 256)
-        sub(4)
-        sub(5)
-        sub(6)
-        sub(7)
-        clamp_s(1, 0, 256)
-        store(1, 0, 256)
-        clamp_v(0, 256, 512)
-        store(0, 256, 512)
-        clamp_v(1, 256, 512)
-        store(1, 256, 512)
+        subtract(blocks[0])
+        subtract(blocks[1])
+        clamp_and_store(blocks[0], on_scalar=False)
+        subtract(blocks[2])
+        subtract(blocks[3])
+        clamp_and_store(blocks[1], on_scalar=True)
+        clamp_and_store(blocks[2], on_scalar=False)
+        clamp_and_store(blocks[3], on_scalar=False)

@@ -23,7 +23,8 @@ PER_COLUMN = 16
 ROWS = 16
 QUADRANT = 32
 K_FIRST = 112
-C_FIRST = 48
+C_FIRST = 4
+C_STEP = 8
 LSE_ROW = P - 2
 C_HEAD = 768
 PIECE = 128
@@ -46,20 +47,18 @@ def tile_attend_dupkl_topk_kernel(tc, qT, k_words, k_scales, c_words, c_scales, 
         k_plane = keep.tile([P, N // PACK], I32, name="k_plane", align_bytes=64)
         c_plane = keep.tile([P, N // PACK], I32, name="c_plane", align_bytes=64)
 
+        nc.vector.memset(cs_pool[:], 0)
         nc.vector.memset(ks_pool[0:K_FIRST, :], 0)
-        nc.vector.memset(cs_pool[0:C_FIRST, :], 0)
-        nc.vector.memset(cs_pool[C_FIRST + ROWS : P, :], 0)
         nc.vector.memset(k_plane[:], 0)
-        nc.vector.memset(c_plane[:], 0)
         nc.gpsimd.memset(lse_rows[0:LSE_ROW, :], 0.0)
         make_identity(nc, ident[:])
 
         nc.sync.dma_start(offsets[:], offs)
         nc.scalar.dma_start(ks_pool[K_FIRST : K_FIRST + ROWS, :], k_scales[0].bitcast(I32))
         nc.sync.dma_start(q_raw[:], qT[0].rearrange("(p j) w -> p j w", j=PACK))
-        nc.sync.dma_start(cs_pool[C_FIRST : C_FIRST + ROWS, :], c_scales[0].bitcast(I32))
         nc.sync.dma_start(lse_rows[LSE_ROW : LSE_ROW + 1, :], ls[0].rearrange("q o -> o q"))
         nc.sync.dma_start(lse_rows[LSE_ROW + 1 : P, :], l2[0].rearrange("q o -> o q"))
+        nc.sync.dma_start(cs_pool[C_FIRST:P:C_STEP, :], c_scales[0].bitcast(I32))
         nc.sync.dma_start(k_pool[:], k_words[0].rearrange("p n t -> p (n t)").bitcast(I32))
         c_rows = c_words[0].rearrange("p n t -> p (n t)").bitcast(I32)
         nc.sync.dma_start(c_head[:], c_rows[:, 0:C_HEAD])
@@ -70,13 +69,13 @@ def tile_attend_dupkl_topk_kernel(tc, qT, k_words, k_scales, c_words, c_scales, 
         neg = keep.tile([P, QT, 2], F32, name="neg", align_bytes=64)
         nc.scalar.mul(neg[:], lse_cols[:, :, LSE_ROW:P], -1.0)
 
-        def move_to_plane(plane, rows, first):
-            for j in range(PACK):
-                nc.sync.dma_start(plane[j:P:QUADRANT, :], rows[first + j : first + ROWS : PACK, :].bitcast(I32))
+        def move_to_plane(plane, rows, first, step, at, moved):
+            for j in moved:
+                nc.sync.dma_start(plane[at + j : P : QUADRANT, :], rows[first + j * step : P : PACK * step, :].bitcast(I32))
 
         ks_rows = keep.tile([P, N], U8, name="ks_rows", align_bytes=64)
         nc.vector.tensor_copy(ks_rows[:], ks_pool[:].bitcast(U8).indirect(offsets[:]))
-        move_to_plane(k_plane, ks_rows, K_FIRST)
+        move_to_plane(k_plane, ks_rows, K_FIRST, 1, 0, range(PACK))
         c_pool = keep.tile([P, T], I32, name="c_pool", tag="ks_then_c", align_bytes=64)
         nc.sync.dma_start(c_pool[:, C_HEAD:T], c_rows[:, C_HEAD:T])
         cs_rows = keep.tile([P, N], U8, name="cs_rows", align_bytes=64)
@@ -84,9 +83,10 @@ def tile_attend_dupkl_topk_kernel(tc, qT, k_words, k_scales, c_words, c_scales, 
 
         q_bf = keep.tile([P, QT, P, PACK], BF16, name="q_bf", align_bytes=64)
         nc.scalar.copy(q_bf[:], q_raw[:].rearrange("p j (t m) -> p t m j", t=QT))
-        move_to_plane(c_plane, cs_rows, C_FIRST)
+        nc.vector.tensor_copy(c_plane[:], cs_rows[:].bitcast(I32))
+        move_to_plane(c_plane, cs_rows, C_FIRST, C_STEP, C_FIRST, range(1, PACK))
         k_bytes = k_plane[:].bitcast(U8)
-        c_bytes = c_plane[:].bitcast(U8)
+        c_bytes = c_plane[C_FIRST:P, :].bitcast(U8)
         q_codes = keep.tile([P, NQ], U32, name="q_codes", tag="cs_then_q", align_bytes=64)
         q_scales = keep.tile([P, NQ], U8, name="q_scales", align_bytes=64)
         nc.vector.quantize_mx(

@@ -26,7 +26,7 @@ K_FIRST = 112
 C_FIRST = 4
 C_STEP = 8
 LSE_ROW = P - 2
-C_HEAD = 768
+C_HEAD = 512
 PIECE = 128
 
 
@@ -63,7 +63,7 @@ def tile_attend_dupkl_topk_kernel(tc, qT, k_words, k_scales, c_words, c_scales, 
         c_rows = c_words[0].rearrange("p n t -> p (n t)").bitcast(I32)
         nc.sync.dma_start(c_head[:], c_rows[:, 0:C_HEAD])
 
-        lse_cols = psum.tile([P, QT, P], F32, name="lse_cols")
+        lse_cols = psum.tile([P, QT, P], F32, name="lse_cols", tag="lse_then_z")
         for t in range(QT):
             nc.tensor.transpose(lse_cols[:, t, :], lse_rows[:, t * P : (t + 1) * P], ident[:])
         neg = keep.tile([P, QT, 2], F32, name="neg", align_bytes=64)
@@ -133,9 +133,10 @@ def tile_attend_dupkl_topk_kernel(tc, qT, k_words, k_scales, c_words, c_scales, 
         blocks = [(h, t) for h in range(2) for t in range(QT)]
         ez = {}
         for b, (h, t) in enumerate(blocks):
-            width = PIECE if b == 0 else HALF
+            width = PIECE if t == 0 else HALF
             for n0 in range(h * HALF, (h + 1) * HALF, width):
-                z = psum.tile([P, width], F32, name=f"z{t}_{n0}")
+                tag = "lse_then_z" if b == len(blocks) - 1 else f"z{t}_{n0}"
+                z = psum.tile([P, width], F32, name=f"z{t}_{n0}", tag=tag)
                 product(z[:], t, cw, c_bytes, n0, width)
                 for at in range(0, width, PIECE):
                     piece = keep.tile([P, PIECE], F32, name=f"ez{t}_{n0 + at}", align_bytes=64)

@@ -22,9 +22,9 @@ HALF = N // 2
 PER_COLUMN = 16
 ROWS = 16
 QUADRANT = 32
-K_FIRST = 112
+K_FIRST = P - ROWS
 C_FIRST = 4
-C_STEP = 8
+C_STEP = QUADRANT // PACK
 LSE_ROW = P - 2
 C_HEAD = 512
 PIECE = 128
@@ -56,8 +56,8 @@ def tile_attend_dupkl_topk_kernel(tc, qT, k_words, k_scales, c_words, c_scales, 
         nc.sync.dma_start(offsets[:], offs)
         nc.scalar.dma_start(ks_pool[K_FIRST : K_FIRST + ROWS, :], k_scales[0].bitcast(I32))
         nc.sync.dma_start(q_raw[:], qT[0].rearrange("(p j) w -> p j w", j=PACK))
-        nc.sync.dma_start(lse_rows[LSE_ROW : LSE_ROW + 1, :], ls[0].rearrange("q o -> o q"))
-        nc.sync.dma_start(lse_rows[LSE_ROW + 1 : P, :], l2[0].rearrange("q o -> o q"))
+        nc.scalar.dma_start(lse_rows[LSE_ROW : LSE_ROW + 1, :], ls[0].rearrange("q o -> o q"))
+        nc.scalar.dma_start(lse_rows[LSE_ROW + 1 : P, :], l2[0].rearrange("q o -> o q"))
         nc.sync.dma_start(cs_pool[C_FIRST:P:C_STEP, :], c_scales[0].bitcast(I32))
         nc.sync.dma_start(k_pool[:], k_words[0].rearrange("p n t -> p (n t)").bitcast(I32))
         c_rows = c_words[0].rearrange("p n t -> p (n t)").bitcast(I32)
@@ -69,13 +69,14 @@ def tile_attend_dupkl_topk_kernel(tc, qT, k_words, k_scales, c_words, c_scales, 
         neg = keep.tile([P, QT, 2], F32, name="neg", align_bytes=64)
         nc.scalar.mul(neg[:], lse_cols[:, :, LSE_ROW:P], -1.0)
 
-        def move_to_plane(plane, rows, first, step, at, moved):
-            for j in moved:
-                nc.sync.dma_start(plane[at + j : P : QUADRANT, :], rows[first + j * step : P : PACK * step, :].bitcast(I32))
+        def move_rows(plane, start, rows, first, step, places):
+            for j in places:
+                source = rows[first + j * step : P : PACK * step, :].bitcast(I32)
+                nc.sync.dma_start(plane[start + j : P : QUADRANT, :], source)
 
         ks_rows = keep.tile([P, N], U8, name="ks_rows", align_bytes=64)
         nc.vector.tensor_copy(ks_rows[:], ks_pool[:].bitcast(U8).indirect(offsets[:]))
-        move_to_plane(k_plane, ks_rows, K_FIRST, 1, 0, range(PACK))
+        move_rows(k_plane, 0, ks_rows, K_FIRST, 1, range(PACK))
         c_pool = keep.tile([P, T], I32, name="c_pool", tag="ks_then_c", align_bytes=64)
         nc.sync.dma_start(c_pool[:, C_HEAD:T], c_rows[:, C_HEAD:T])
         cs_rows = keep.tile([P, N], U8, name="cs_rows", align_bytes=64)
@@ -83,8 +84,9 @@ def tile_attend_dupkl_topk_kernel(tc, qT, k_words, k_scales, c_words, c_scales, 
 
         q_bf = keep.tile([P, QT, P, PACK], BF16, name="q_bf", align_bytes=64)
         nc.scalar.copy(q_bf[:], q_raw[:].rearrange("p j (t m) -> p t m j", t=QT))
+
         nc.vector.tensor_copy(c_plane[:], cs_rows[:].bitcast(I32))
-        move_to_plane(c_plane, cs_rows, C_FIRST, C_STEP, C_FIRST, range(1, PACK))
+        move_rows(c_plane, C_FIRST, cs_rows, C_FIRST, C_STEP, range(1, PACK))
         k_bytes = k_plane[:].bitcast(U8)
         c_bytes = c_plane[C_FIRST:P, :].bitcast(U8)
         q_codes = keep.tile([P, NQ], U32, name="q_codes", tag="cs_then_q", align_bytes=64)
@@ -132,10 +134,10 @@ def tile_attend_dupkl_topk_kernel(tc, qT, k_words, k_scales, c_words, c_scales, 
         cw = gather_words(c_pool, "cw")
         blocks = [(h, t) for h in range(2) for t in range(QT)]
         ez = {}
-        for b, (h, t) in enumerate(blocks):
+        for h, t in blocks:
             width = PIECE if t == 0 else HALF
             for n0 in range(h * HALF, (h + 1) * HALF, width):
-                tag = "lse_then_z" if b == len(blocks) - 1 else f"z{t}_{n0}"
+                tag = "lse_then_z" if (h, t) == blocks[-1] else f"z{t}_{n0}"
                 z = psum.tile([P, width], F32, name=f"z{t}_{n0}", tag=tag)
                 product(z[:], t, cw, c_bytes, n0, width)
                 for at in range(0, width, PIECE):

@@ -26,7 +26,7 @@ K_FIRST = P - ROWS
 C_FIRST = 4
 C_STEP = QUADRANT // PACK
 LSE_ROW = P - 2
-C_HEAD = 512
+C_HEAD = 640
 PIECE = 128
 
 

@@ -27,6 +27,7 @@ C_FIRST = 4
 C_STEP = QUADRANT // PACK
 LSE_ROW = P - 2
 C_HEAD = 640
+LAST = 64
 PIECE = 128
 
 
@@ -133,41 +134,42 @@ def tile_attend_dupkl_topk_kernel(tc, qT, k_words, k_scales, c_words, c_scales, 
 
         cw = gather_words(c_pool, "cw")
         blocks = [(h, t) for h in range(2) for t in range(QT)]
-        ez = {}
+        ez = keep.tile([P, QT, N], F32, name="ez", align_bytes=64)
         for h, t in blocks:
             width = PIECE if t == 0 else HALF
             for n0 in range(h * HALF, (h + 1) * HALF, width):
                 tag = "lse_then_z" if (h, t) == blocks[-1] else f"z{t}_{n0}"
                 z = psum.tile([P, width], F32, name=f"z{t}_{n0}", tag=tag)
                 product(z[:], t, cw, c_bytes, n0, width)
-                for at in range(0, width, PIECE):
-                    piece = keep.tile([P, PIECE], F32, name=f"ez{t}_{n0 + at}", align_bytes=64)
-                    nc.scalar.activation(piece[:], z[:, at : at + PIECE], ACT.Exp, bias=neg[:, t, 1:2])
-                    ez[(t, n0 + at)] = piece
+                cuts = [0, width - LAST, width] if (h, t) == blocks[-1] else list(range(0, width + 1, PIECE))
+                for lo, hi in zip(cuts, cuts[1:]):
+                    nc.scalar.activation(ez[:, t, n0 + lo : n0 + hi], z[:, lo:hi], ACT.Exp, bias=neg[:, t, 1:2])
 
         out_tiles = out[0].rearrange("(t p) n -> p t n", t=QT)
         diff = keep.tile([P, QT, N], F32, name="diff", align_bytes=64)
         res = keep.tile([P, QT, N], F32, name="res", align_bytes=64)
 
-        def subtract(block):
-            h, t = block
-            for n0 in range(h * HALF, (h + 1) * HALF, PIECE):
-                nc.vector.tensor_sub(diff[:, t, n0 : n0 + PIECE], ea[:, t, n0 : n0 + PIECE], ez[(t, n0)][:])
+        def subtract(t, lo, hi):
+            nc.vector.tensor_sub(diff[:, t, lo:hi], ea[:, t, lo:hi], ez[:, t, lo:hi])
 
-        def clamp_and_store(block, on_scalar):
-            h, t = block
-            cols = slice(h * HALF, (h + 1) * HALF)
-            if on_scalar:
-                nc.scalar.activation(res[:, t, cols], diff[:, t, cols], ACT.Relu)
-            else:
-                nc.vector.tensor_scalar_max(res[:, t, cols], diff[:, t, cols], 0.0)
-            nc.sync.dma_start(out_tiles[:, t, cols], res[:, t, cols])
+        def clamp(t, lo, hi):
+            nc.vector.tensor_scalar_max(res[:, t, lo:hi], diff[:, t, lo:hi], 0.0)
 
-        subtract(blocks[0])
-        subtract(blocks[1])
-        clamp_and_store(blocks[0], on_scalar=False)
-        subtract(blocks[2])
-        subtract(blocks[3])
-        clamp_and_store(blocks[1], on_scalar=True)
-        clamp_and_store(blocks[2], on_scalar=False)
-        clamp_and_store(blocks[3], on_scalar=False)
+        def store(t, lo, hi):
+            nc.sync.dma_start(out_tiles[:, t, lo:hi], res[:, t, lo:hi])
+
+        for t in range(QT):
+            subtract(t, 0, PIECE)
+            subtract(t, PIECE, HALF)
+        clamp(0, 0, HALF)
+        store(0, 0, HALF)
+        subtract(0, HALF, HALF + PIECE)
+        subtract(0, HALF + PIECE, N)
+        subtract(1, HALF, N - LAST)
+        subtract(1, N - LAST, N)
+        nc.scalar.activation(res[:, 1, 0:HALF], diff[:, 1, 0:HALF], ACT.Relu)
+        store(1, 0, HALF)
+        clamp(0, HALF, N)
+        store(0, HALF, N)
+        clamp(1, HALF, N)
+        store(1, HALF, N)

@@ -14,6 +14,7 @@ U16 = mybir.dt.uint16
 U8 = mybir.dt.uint8
 FP8X4 = mybir.dt.float8_e4m3fn_x4
 ACT = mybir.ActivationFunctionType
+ALU = mybir.AluOpType
 
 P = 128
 PACK = 4
@@ -27,7 +28,6 @@ C_FIRST = 4
 C_STEP = QUADRANT // PACK
 LSE_ROW = P - 2
 C_HEAD = 640
-LAST = 64
 PIECE = 128
 
 
@@ -98,6 +98,14 @@ def tile_attend_dupkl_topk_kernel(tc, qT, k_words, k_scales, c_words, c_scales, 
             in_=q_bf[:].rearrange("p t m j -> p (t m j)"),
         )
 
+        minus_bf = keep.tile([P, P * PACK], BF16, name="minus_bf", align_bytes=64)
+        nc.scalar.mul(minus_bf[:], q_bf[:, QT - 1].rearrange("p m j -> p (m j)"), -1.0)
+        minus_codes = keep.tile([P, P], U32, name="minus_codes", align_bytes=64)
+        minus_scales = keep.tile([P, P], U8, name="minus_scales", align_bytes=64)
+        nc.vector.quantize_mx(out=minus_codes[:].bitcast(FP8X4), scales=minus_scales[:], in_=minus_bf[:])
+        lse_gap = keep.tile([P, 1], F32, name="lse_gap", align_bytes=64)
+        nc.vector.tensor_sub(lse_gap[:], neg[:, QT - 1, 0:1], neg[:, QT - 1, 1:2])
+
         def gather_words(pool, name):
             halves = []
             for h in range(2):
@@ -132,18 +140,47 @@ def tile_attend_dupkl_topk_kernel(tc, qT, k_words, k_scales, c_words, c_scales, 
                     ea[:, t, h * HALF : (h + 1) * HALF], a[h][:, t, :], ACT.Exp, bias=neg[:, t, 0:1]
                 )
 
+        last = QT - 1
+        gap = psum.tile([P, HALF], F32, name="gap", tag="lse_then_z")
+        nc.tensor.matmul_mx(
+            out=gap[:],
+            lhsT=q_codes[:, last * P : (last + 1) * P].bitcast(FP8X4),
+            lhsT_scale=q_scales[:, last * P : (last + 1) * P],
+            rhs=kw[1][:].bitcast(FP8X4),
+            rhs_scale=k_bytes[:, HALF:N],
+            start=True,
+            stop=False,
+        )
+        minus_ea = keep.tile([P, HALF], F32, name="minus_ea", align_bytes=64)
+        nc.scalar.mul(minus_ea[:], ea[:, last, HALF:N], -1.0)
+
         cw = gather_words(c_pool, "cw")
         blocks = [(h, t) for h in range(2) for t in range(QT)]
         ez = keep.tile([P, QT, N], F32, name="ez", align_bytes=64)
-        for h, t in blocks:
+        for h, t in blocks[:-1]:
             width = PIECE if t == 0 else HALF
             for n0 in range(h * HALF, (h + 1) * HALF, width):
-                tag = "lse_then_z" if (h, t) == blocks[-1] else f"z{t}_{n0}"
-                z = psum.tile([P, width], F32, name=f"z{t}_{n0}", tag=tag)
+                z = psum.tile([P, width], F32, name=f"z{t}_{n0}")
                 product(z[:], t, cw, c_bytes, n0, width)
-                cuts = [0, width - LAST, width] if (h, t) == blocks[-1] else list(range(0, width + 1, PIECE))
-                for lo, hi in zip(cuts, cuts[1:]):
-                    nc.scalar.activation(ez[:, t, n0 + lo : n0 + hi], z[:, lo:hi], ACT.Exp, bias=neg[:, t, 1:2])
+                for lo in range(0, width, PIECE):
+                    nc.scalar.activation(
+                        ez[:, t, n0 + lo : n0 + lo + PIECE], z[:, lo : lo + PIECE], ACT.Exp, bias=neg[:, t, 1:2]
+                    )
+        nc.tensor.matmul_mx(
+            out=gap[:],
+            lhsT=minus_codes[:].bitcast(FP8X4),
+            lhsT_scale=minus_scales[:],
+            rhs=cw[1][:].bitcast(FP8X4),
+            rhs_scale=c_bytes[:, HALF:N],
+            start=False,
+            stop=True,
+        )
+        lead = keep.tile([P, HALF], F32, name="lead", align_bytes=64)
+        ratio = keep.tile([P, HALF], F32, name="ratio", align_bytes=64)
+        for lo in range(0, HALF, PIECE):
+            nc.scalar.activation(lead[:, lo : lo + PIECE], gap[:, lo : lo + PIECE], ACT.Relu, bias=lse_gap[:])
+        for lo in range(0, HALF, PIECE):
+            nc.scalar.activation(ratio[:, lo : lo + PIECE], lead[:, lo : lo + PIECE], ACT.Exp, scale=-1.0)
 
         out_tiles = out[0].rearrange("(t p) n -> p t n", t=QT)
         diff = keep.tile([P, QT, N], F32, name="diff", align_bytes=64)
@@ -155,21 +192,26 @@ def tile_attend_dupkl_topk_kernel(tc, qT, k_words, k_scales, c_words, c_scales, 
         def clamp(t, lo, hi):
             nc.vector.tensor_scalar_max(res[:, t, lo:hi], diff[:, t, lo:hi], 0.0)
 
+        def finish(lo, hi):
+            nc.vector.scalar_tensor_tensor(
+                res[:, last, HALF + lo : HALF + hi], ratio[:, lo:hi], 1.0, minus_ea[:, lo:hi], ALU.subtract, ALU.mult
+            )
+
         def store(t, lo, hi):
             nc.sync.dma_start(out_tiles[:, t, lo:hi], res[:, t, lo:hi])
 
-        for t in range(QT):
-            subtract(t, 0, PIECE)
-            subtract(t, PIECE, HALF)
+        subtract(0, 0, PIECE)
+        subtract(0, PIECE, HALF)
+        subtract(1, 0, PIECE)
+        subtract(1, PIECE, HALF)
         clamp(0, 0, HALF)
         store(0, 0, HALF)
         subtract(0, HALF, HALF + PIECE)
         subtract(0, HALF + PIECE, N)
-        subtract(1, HALF, N - LAST)
-        subtract(1, N - LAST, N)
-        nc.scalar.activation(res[:, 1, 0:HALF], diff[:, 1, 0:HALF], ACT.Relu)
+        clamp(1, 0, HALF)
         store(1, 0, HALF)
         clamp(0, HALF, N)
         store(0, HALF, N)
-        clamp(1, HALF, N)
+        finish(0, PIECE)
+        finish(PIECE, HALF)
         store(1, HALF, N)

@@ -28,6 +28,7 @@ C_FIRST = 4
 C_STEP = QUADRANT // PACK
 LSE_ROW = P - 2
 C_HEAD = 640
+LAST = 64
 PIECE = 128
 
 
@@ -155,17 +156,33 @@ def tile_attend_dupkl_topk_kernel(tc, qT, k_words, k_scales, c_words, c_scales, 
         nc.scalar.mul(minus_ea[:], ea[:, last, HALF:N], -1.0)
 
         cw = gather_words(c_pool, "cw")
-        blocks = [(h, t) for h in range(2) for t in range(QT)]
         ez = keep.tile([P, QT, N], F32, name="ez", align_bytes=64)
-        for h, t in blocks[:-1]:
-            width = PIECE if t == 0 else HALF
-            for n0 in range(h * HALF, (h + 1) * HALF, width):
-                z = psum.tile([P, width], F32, name=f"z{t}_{n0}")
-                product(z[:], t, cw, c_bytes, n0, width)
-                for lo in range(0, width, PIECE):
-                    nc.scalar.activation(
-                        ez[:, t, n0 + lo : n0 + lo + PIECE], z[:, lo : lo + PIECE], ACT.Exp, bias=neg[:, t, 1:2]
-                    )
+        lead = keep.tile([P, HALF], F32, name="lead", align_bytes=64)
+        ratio = keep.tile([P, HALF], F32, name="ratio", align_bytes=64)
+
+        def draft(t, n0, width):
+            z = psum.tile([P, width], F32, name=f"z{t}_{n0}")
+            product(z[:], t, cw, c_bytes, n0, width)
+            return z
+
+        def exp_draft(z, t, n0, lo):
+            nc.scalar.activation(
+                ez[:, t, n0 + lo : n0 + lo + PIECE], z[:, lo : lo + PIECE], ACT.Exp, bias=neg[:, t, 1:2]
+            )
+
+        def relu_gap(lo, hi):
+            nc.scalar.activation(lead[:, lo:hi], gap[:, lo:hi], ACT.Relu, bias=lse_gap[:])
+
+        def exp_gap(lo, hi):
+            nc.scalar.activation(ratio[:, lo:hi], lead[:, lo:hi], ACT.Exp, scale=-1.0)
+
+        for n0 in (0, PIECE):
+            exp_draft(draft(0, n0, PIECE), 0, n0, 0)
+        z = draft(1, 0, HALF)
+        for lo in (0, PIECE):
+            exp_draft(z, 1, 0, lo)
+        for n0 in (HALF, HALF + PIECE):
+            exp_draft(draft(0, n0, PIECE), 0, n0, 0)
         nc.tensor.matmul_mx(
             out=gap[:],
             lhsT=minus_codes[:].bitcast(FP8X4),
@@ -175,12 +192,12 @@ def tile_attend_dupkl_topk_kernel(tc, qT, k_words, k_scales, c_words, c_scales, 
             start=False,
             stop=True,
         )
-        lead = keep.tile([P, HALF], F32, name="lead", align_bytes=64)
-        ratio = keep.tile([P, HALF], F32, name="ratio", align_bytes=64)
-        for lo in range(0, HALF, PIECE):
-            nc.scalar.activation(lead[:, lo : lo + PIECE], gap[:, lo : lo + PIECE], ACT.Relu, bias=lse_gap[:])
-        for lo in range(0, HALF, PIECE):
-            nc.scalar.activation(ratio[:, lo : lo + PIECE], lead[:, lo : lo + PIECE], ACT.Exp, scale=-1.0)
+        wide = HALF - LAST
+        cuts = [(0, wide // 2), (wide // 2, wide), (wide, HALF)]
+        for lo, hi in cuts:
+            relu_gap(lo, hi)
+        for lo, hi in cuts:
+            exp_gap(lo, hi)
 
         out_tiles = out[0].rearrange("(t p) n -> p t n", t=QT)
         diff = keep.tile([P, QT, N], F32, name="diff", align_bytes=64)
@@ -197,21 +214,22 @@ def tile_attend_dupkl_topk_kernel(tc, qT, k_words, k_scales, c_words, c_scales, 
                 res[:, last, HALF + lo : HALF + hi], ratio[:, lo:hi], 1.0, minus_ea[:, lo:hi], ALU.subtract, ALU.mult
             )
 
-        def store(t, lo, hi):
-            nc.sync.dma_start(out_tiles[:, t, lo:hi], res[:, t, lo:hi])
+        def store(t, lo, hi, parts=1):
+            for first in range(parts):
+                nc.sync.dma_start(out_tiles[first:P:parts, t, lo:hi], res[first:P:parts, t, lo:hi])
 
         subtract(0, 0, PIECE)
         subtract(0, PIECE, HALF)
         subtract(1, 0, PIECE)
         subtract(1, PIECE, HALF)
         clamp(0, 0, HALF)
-        store(0, 0, HALF)
+        store(0, 0, HALF, 2)
         subtract(0, HALF, HALF + PIECE)
         subtract(0, HALF + PIECE, N)
         clamp(1, 0, HALF)
         store(1, 0, HALF)
         clamp(0, HALF, N)
         store(0, HALF, N)
-        finish(0, PIECE)
-        finish(PIECE, HALF)
+        finish(0, wide)
+        finish(wide, HALF)
         store(1, HALF, N)

@@ -131,27 +131,24 @@ def tile_attend_dupkl_topk_kernel(tc, qT, k_words, k_scales, c_words, c_scales, 
         kw = gather_words(k_pool, "kw")
         nc.vector.tensor_copy(c_pool[:, 0:C_HEAD], c_head[:])
         ea = keep.tile([P, QT, N], F32, name="ea", align_bytes=64)
-        a = [psum.tile([P, QT, HALF], F32, name=f"a{h}") for h in range(2)]
         for h in range(2):
-            for t in range(QT):
-                product(a[h][:, t, :], t, kw, k_bytes, h * HALF, HALF)
-        for h in range(2):
-            for t in range(QT):
-                nc.scalar.activation(
-                    ea[:, t, h * HALF : (h + 1) * HALF], a[h][:, t, :], ACT.Exp, bias=neg[:, t, 0:1]
-                )
+            for t in reversed(range(QT)):
+                a = psum.tile([P, HALF], F32, name=f"a{h}{t}", tag=f"scores{t}_{h}")
+                product(a[:], t, kw, k_bytes, h * HALF, HALF)
+                nc.scalar.activation(ea[:, t, h * HALF : (h + 1) * HALF], a[:], ACT.Exp, bias=neg[:, t, 0:1])
 
         last = QT - 1
-        gap = psum.tile([P, HALF], F32, name="gap", tag="lse_then_z")
-        nc.tensor.matmul_mx(
-            out=gap[:],
-            lhsT=q_codes[:, last * P : (last + 1) * P].bitcast(FP8X4),
-            lhsT_scale=q_scales[:, last * P : (last + 1) * P],
-            rhs=kw[1][:].bitcast(FP8X4),
-            rhs_scale=k_bytes[:, HALF:N],
-            start=True,
-            stop=False,
-        )
+        gap = [psum.tile([P, PIECE], F32, name=f"gap{i}", tag=("lse_then_z", "scores1_0")[i]) for i in range(2)]
+        for i in range(2):
+            nc.tensor.matmul_mx(
+                out=gap[i][:],
+                lhsT=q_codes[:, last * P : (last + 1) * P].bitcast(FP8X4),
+                lhsT_scale=q_scales[:, last * P : (last + 1) * P],
+                rhs=kw[1][:, i * PIECE : (i + 1) * PIECE].bitcast(FP8X4),
+                rhs_scale=k_bytes[:, HALF + i * PIECE : HALF + (i + 1) * PIECE],
+                start=True,
+                stop=False,
+            )
         minus_ea = keep.tile([P, HALF], F32, name="minus_ea", align_bytes=64)
         nc.scalar.mul(minus_ea[:], ea[:, last, HALF:N], -1.0)
 
@@ -161,7 +158,9 @@ def tile_attend_dupkl_topk_kernel(tc, qT, k_words, k_scales, c_words, c_scales, 
         ratio = keep.tile([P, HALF], F32, name="ratio", align_bytes=64)
 
         def draft(t, n0, width):
-            z = psum.tile([P, width], F32, name=f"z{t}_{n0}")
+            place = (n0 % HALF) // PIECE + 2 * t + 4 * (n0 // HALF)
+            tag = f"z{place}" if place < 3 else ("scores0_1", "scores0_0", "scores1_1")[place - 3]
+            z = psum.tile([P, width], F32, name=f"z{t}_{n0}", tag=tag)
             product(z[:], t, cw, c_bytes, n0, width)
             return z
 
@@ -171,29 +170,28 @@ def tile_attend_dupkl_topk_kernel(tc, qT, k_words, k_scales, c_words, c_scales, 
             )
 
         def relu_gap(lo, hi):
-            nc.scalar.activation(lead[:, lo:hi], gap[:, lo:hi], ACT.Relu, bias=lse_gap[:])
+            nc.scalar.activation(lead[:, lo:hi], gap[lo // PIECE][:, lo % PIECE : (hi - 1) % PIECE + 1], ACT.Relu, bias=lse_gap[:])
 
         def exp_gap(lo, hi):
             nc.scalar.activation(ratio[:, lo:hi], lead[:, lo:hi], ACT.Exp, scale=-1.0)
 
-        for n0 in (0, PIECE):
-            exp_draft(draft(0, n0, PIECE), 0, n0, 0)
-        z = draft(1, 0, HALF)
-        for lo in (0, PIECE):
-            exp_draft(z, 1, 0, lo)
+        for t in range(QT):
+            for n0 in (0, PIECE):
+                exp_draft(draft(t, n0, PIECE), t, n0, 0)
         for n0 in (HALF, HALF + PIECE):
             exp_draft(draft(0, n0, PIECE), 0, n0, 0)
-        nc.tensor.matmul_mx(
-            out=gap[:],
-            lhsT=minus_codes[:].bitcast(FP8X4),
-            lhsT_scale=minus_scales[:],
-            rhs=cw[1][:].bitcast(FP8X4),
-            rhs_scale=c_bytes[:, HALF:N],
-            start=False,
-            stop=True,
-        )
+        for i in range(2):
+            nc.tensor.matmul_mx(
+                out=gap[i][:],
+                lhsT=minus_codes[:].bitcast(FP8X4),
+                lhsT_scale=minus_scales[:],
+                rhs=cw[1][:, i * PIECE : (i + 1) * PIECE].bitcast(FP8X4),
+                rhs_scale=c_bytes[:, HALF + i * PIECE : HALF + (i + 1) * PIECE],
+                start=False,
+                stop=True,
+            )
         wide = HALF - LAST
-        cuts = [(0, wide // 2), (wide // 2, wide), (wide, HALF)]
+        cuts = [(0, PIECE), (PIECE, wide), (wide, HALF)]
         for lo, hi in cuts:
             relu_gap(lo, hi)
         for lo, hi in cuts:

@@ -23,11 +23,12 @@ HALF = N // 2
 PER_COLUMN = 16
 ROWS = 16
 QUADRANT = 32
-K_FIRST = P - ROWS
-C_FIRST = 4
-C_STEP = QUADRANT // PACK
+K_FIRST = 2 * QUADRANT - ROWS
+C_FIRST = 2 * QUADRANT
+C_STEP = PACK
+C_PLANE = 4
 LSE_ROW = P - 2
-C_HEAD = 640
+C_HEAD = 512
 LAST = 64
 PIECE = 128
 
@@ -51,7 +52,9 @@ def tile_attend_dupkl_topk_kernel(tc, qT, k_words, k_scales, c_words, c_scales, 
 
         nc.vector.memset(cs_pool[:], 0)
         nc.vector.memset(ks_pool[0:K_FIRST, :], 0)
+        nc.vector.memset(ks_pool[K_FIRST + ROWS : P, :], 0)
         nc.vector.memset(k_plane[:], 0)
+        nc.vector.memset(c_plane[:], 0)
         nc.gpsimd.memset(lse_rows[0:LSE_ROW, :], 0.0)
         make_identity(nc, ident[:])
 
@@ -73,7 +76,7 @@ def tile_attend_dupkl_topk_kernel(tc, qT, k_words, k_scales, c_words, c_scales, 
 
         def move_rows(plane, start, rows, first, step, places):
             for j in places:
-                source = rows[first + j * step : P : PACK * step, :].bitcast(I32)
+                source = rows[first + j * step : first + ROWS * step : PACK * step, :].bitcast(I32)
                 nc.sync.dma_start(plane[start + j : P : QUADRANT, :], source)
 
         ks_rows = keep.tile([P, N], U8, name="ks_rows", align_bytes=64)
@@ -87,10 +90,9 @@ def tile_attend_dupkl_topk_kernel(tc, qT, k_words, k_scales, c_words, c_scales, 
         q_bf = keep.tile([P, QT, P, PACK], BF16, name="q_bf", align_bytes=64)
         nc.scalar.copy(q_bf[:], q_raw[:].rearrange("p j (t m) -> p t m j", t=QT))
 
-        nc.vector.tensor_copy(c_plane[:], cs_rows[:].bitcast(I32))
-        move_rows(c_plane, C_FIRST, cs_rows, C_FIRST, C_STEP, range(1, PACK))
+        move_rows(c_plane, C_PLANE, cs_rows, C_FIRST, C_STEP, range(PACK))
         k_bytes = k_plane[:].bitcast(U8)
-        c_bytes = c_plane[C_FIRST:P, :].bitcast(U8)
+        c_bytes = c_plane[C_PLANE:P, :].bitcast(U8)
         q_codes = keep.tile([P, NQ], U32, name="q_codes", tag="cs_then_q", align_bytes=64)
         q_scales = keep.tile([P, NQ], U8, name="q_scales", align_bytes=64)
         nc.vector.quantize_mx(
@@ -221,7 +223,7 @@ def tile_attend_dupkl_topk_kernel(tc, qT, k_words, k_scales, c_words, c_scales, 
         subtract(1, 0, PIECE)
         subtract(1, PIECE, HALF)
         clamp(0, 0, HALF)
-        store(0, 0, HALF, 2)
+        store(0, 0, HALF)
         subtract(0, HALF, HALF + PIECE)
         subtract(0, HALF + PIECE, N)
         clamp(1, 0, HALF)

@@ -109,102 +109,86 @@ def tile_attend_dupkl_topk_kernel(tc, qT, k_words, k_scales, c_words, c_scales, 
         lse_gap = keep.tile([P, 1], F32, name="lse_gap", align_bytes=64)
         nc.vector.tensor_sub(lse_gap[:], neg[:, QT - 1, 0:1], neg[:, QT - 1, 1:2])
 
-        def gather_words(pool, name):
-            halves = []
-            for h in range(2):
-                words = keep.tile([P, HALF], U32, name=f"{name}{h}", align_bytes=64)
-                entries = offsets[:, h * HALF // PER_COLUMN : (h + 1) * HALF // PER_COLUMN]
+        def gather_words(pool, name, width):
+            runs = []
+            for n0 in range(0, N, width):
+                words = keep.tile([P, width], U32, name=f"{name}{n0}", align_bytes=64)
+                entries = offsets[:, n0 // PER_COLUMN : (n0 + width) // PER_COLUMN]
                 nc.vector.tensor_copy(words[:], pool[:].bitcast(U32).indirect(entries))
-                halves.append(words)
-            return halves
+                runs.append(words)
+            return runs
 
-        def product(scores, t, halves, scale_bytes, n0, width):
-            h, at = divmod(n0, HALF)
+        def product(scores, codes, scales, words, scale_bytes, start=True, stop=True):
             nc.tensor.matmul_mx(
                 out=scores,
-                lhsT=q_codes[:, t * P : (t + 1) * P].bitcast(FP8X4),
-                lhsT_scale=q_scales[:, t * P : (t + 1) * P],
-                rhs=halves[h][:, at : at + width].bitcast(FP8X4),
-                rhs_scale=scale_bytes[:, n0 : n0 + width],
-                start=True,
-                stop=True,
+                lhsT=codes.bitcast(FP8X4),
+                lhsT_scale=scales,
+                rhs=words.bitcast(FP8X4),
+                rhs_scale=scale_bytes,
+                start=start,
+                stop=stop,
             )
 
-        kw = gather_words(k_pool, "kw")
+        def queries(t):
+            return q_codes[:, t * P : (t + 1) * P], q_scales[:, t * P : (t + 1) * P]
+
+        kw = gather_words(k_pool, "kw", HALF)
         nc.vector.tensor_copy(c_pool[:, 0:C_HEAD], c_head[:])
         ea = keep.tile([P, QT, N], F32, name="ea", align_bytes=64)
         for h in range(2):
             for t in reversed(range(QT)):
                 a = psum.tile([P, HALF], F32, name=f"a{h}{t}", tag=f"scores{t}_{h}")
-                product(a[:], t, kw, k_bytes, h * HALF, HALF)
+                product(a[:], *queries(t), kw[h][:], k_bytes[:, h * HALF : (h + 1) * HALF])
                 nc.scalar.activation(ea[:, t, h * HALF : (h + 1) * HALF], a[:], ACT.Exp, bias=neg[:, t, 0:1])
 
         last = QT - 1
-        gap = [psum.tile([P, PIECE], F32, name=f"gap{i}", tag=("lse_then_z", "scores1_0")[i]) for i in range(2)]
-        for i in range(2):
-            nc.tensor.matmul_mx(
-                out=gap[i][:],
-                lhsT=q_codes[:, last * P : (last + 1) * P].bitcast(FP8X4),
-                lhsT_scale=q_scales[:, last * P : (last + 1) * P],
-                rhs=kw[1][:, i * PIECE : (i + 1) * PIECE].bitcast(FP8X4),
-                rhs_scale=k_bytes[:, HALF + i * PIECE : HALF + (i + 1) * PIECE],
-                start=True,
-                stop=False,
-            )
+        gap = {}
+        for b, tag in ((2, "lse_then_z"), (3, "scores1_0")):
+            gap[b] = psum.tile([P, PIECE], F32, name=f"gap{b}", tag=tag)
+            at = b * PIECE - HALF
+            product(gap[b][:], *queries(last), kw[1][:, at : at + PIECE], k_bytes[:, b * PIECE : (b + 1) * PIECE], stop=False)
         minus_ea = keep.tile([P, HALF], F32, name="minus_ea", align_bytes=64)
         nc.scalar.mul(minus_ea[:], ea[:, last, HALF:N], -1.0)
 
-        cw = gather_words(c_pool, "cw")
+        cw = gather_words(c_pool, "cw", PIECE)
         ez = keep.tile([P, QT, N], F32, name="ez", align_bytes=64)
         lead = keep.tile([P, HALF], F32, name="lead", align_bytes=64)
         ratio = keep.tile([P, HALF], F32, name="ratio", align_bytes=64)
+        banks = ["z0", "z1", "z2", "scores0_1", "scores0_0", "scores1_1"]
 
-        def draft(t, n0, width):
-            place = (n0 % HALF) // PIECE + 2 * t + 4 * (n0 // HALF)
-            tag = f"z{place}" if place < 3 else ("scores0_1", "scores0_0", "scores1_1")[place - 3]
-            z = psum.tile([P, width], F32, name=f"z{t}_{n0}", tag=tag)
-            product(z[:], t, cw, c_bytes, n0, width)
-            return z
+        def exp_draft(t, b):
+            cols = slice(b * PIECE, (b + 1) * PIECE)
+            z = psum.tile([P, PIECE], F32, name=f"z{t}_{b}", tag=banks.pop(0))
+            product(z[:], *queries(t), cw[b][:], c_bytes[:, cols])
+            nc.scalar.activation(ez[:, t, cols], z[:], ACT.Exp, bias=neg[:, t, 1:2])
 
-        def exp_draft(z, t, n0, lo):
-            nc.scalar.activation(
-                ez[:, t, n0 + lo : n0 + lo + PIECE], z[:, lo : lo + PIECE], ACT.Exp, bias=neg[:, t, 1:2]
-            )
-
-        def relu_gap(lo, hi):
-            nc.scalar.activation(lead[:, lo:hi], gap[lo // PIECE][:, lo % PIECE : (hi - 1) % PIECE + 1], ACT.Relu, bias=lse_gap[:])
+        def relu_gap(b):
+            product(gap[b][:], minus_codes[:], minus_scales[:], cw[b][:], c_bytes[:, b * PIECE : (b + 1) * PIECE], start=False)
+            at = b * PIECE - HALF
+            nc.scalar.activation(lead[:, at : at + PIECE], gap[b][:], ACT.Relu, bias=lse_gap[:])
 
         def exp_gap(lo, hi):
             nc.scalar.activation(ratio[:, lo:hi], lead[:, lo:hi], ACT.Exp, scale=-1.0)
 
-        for t in range(QT):
-            for n0 in (0, PIECE):
-                exp_draft(draft(t, n0, PIECE), t, n0, 0)
-        for n0 in (HALF, HALF + PIECE):
-            exp_draft(draft(0, n0, PIECE), 0, n0, 0)
-        for i in range(2):
-            nc.tensor.matmul_mx(
-                out=gap[i][:],
-                lhsT=minus_codes[:].bitcast(FP8X4),
-                lhsT_scale=minus_scales[:],
-                rhs=cw[1][:, i * PIECE : (i + 1) * PIECE].bitcast(FP8X4),
-                rhs_scale=c_bytes[:, HALF + i * PIECE : HALF + (i + 1) * PIECE],
-                start=False,
-                stop=True,
-            )
+        for b in range(2):
+            for t in range(QT):
+                exp_draft(t, b)
+        exp_draft(0, 2)
+        relu_gap(2)
+        exp_draft(0, 3)
+        relu_gap(3)
         wide = HALF - LAST
-        cuts = [(0, PIECE), (PIECE, wide), (wide, HALF)]
-        for lo, hi in cuts:
-            relu_gap(lo, hi)
-        for lo, hi in cuts:
-            exp_gap(lo, hi)
+        exp_gap(0, PIECE)
+        exp_gap(PIECE, wide)
+        exp_gap(wide, HALF)
 
         out_tiles = out[0].rearrange("(t p) n -> p t n", t=QT)
         diff = keep.tile([P, QT, N], F32, name="diff", align_bytes=64)
         res = keep.tile([P, QT, N], F32, name="res", align_bytes=64)
 
-        def subtract(t, lo, hi):
-            nc.vector.tensor_sub(diff[:, t, lo:hi], ea[:, t, lo:hi], ez[:, t, lo:hi])
+        def subtract(t, b):
+            cols = slice(b * PIECE, (b + 1) * PIECE)
+            nc.vector.tensor_sub(diff[:, t, cols], ea[:, t, cols], ez[:, t, cols])
 
         def clamp(t, lo, hi):
             nc.vector.tensor_scalar_max(res[:, t, lo:hi], diff[:, t, lo:hi], 0.0)
@@ -214,22 +198,23 @@ def tile_attend_dupkl_topk_kernel(tc, qT, k_words, k_scales, c_words, c_scales, 
                 res[:, last, HALF + lo : HALF + hi], ratio[:, lo:hi], 1.0, minus_ea[:, lo:hi], ALU.subtract, ALU.mult
             )
 
-        def store(t, lo, hi, parts=1):
-            for first in range(parts):
-                nc.sync.dma_start(out_tiles[first:P:parts, t, lo:hi], res[first:P:parts, t, lo:hi])
+        def store(t, lo, hi):
+            nc.sync.dma_start(out_tiles[:, t, lo:hi], res[:, t, lo:hi])
 
-        subtract(0, 0, PIECE)
-        subtract(0, PIECE, HALF)
-        subtract(1, 0, PIECE)
-        subtract(1, PIECE, HALF)
-        clamp(0, 0, HALF)
+        subtract(0, 0)
+        subtract(1, 0)
+        subtract(0, 1)
+        clamp(0, 0, PIECE)
+        subtract(1, 1)
+        clamp(0, PIECE, HALF)
         store(0, 0, HALF)
-        subtract(0, HALF, HALF + PIECE)
-        subtract(0, HALF + PIECE, N)
+        subtract(0, 2)
         clamp(1, 0, HALF)
         store(1, 0, HALF)
+        subtract(0, 3)
+        finish(0, PIECE)
         clamp(0, HALF, N)
         store(0, HALF, N)
-        finish(0, wide)
+        finish(PIECE, wide)
         finish(wide, HALF)
         store(1, HALF, N)

@@ -40,15 +40,15 @@ def tile_attend_dupkl_topk_kernel(tc, qT, k_words, k_scales, c_words, c_scales, 
         psum = ctx.enter_context(tc.psum_pool(name="psum", bufs=1))
 
         offsets = keep.tile([P, N // PER_COLUMN], U16, name="offsets")
-        q_raw = keep.tile([P, PACK, NQ], F32, name="q_raw", align_bytes=64)
-        k_pool = keep.tile([P, T], I32, name="k_pool", align_bytes=64)
-        c_head = keep.tile([P, C_HEAD], I32, name="c_head", align_bytes=64)
-        ks_pool = keep.tile([P, T // PACK], I32, name="ks_pool", tag="ks_then_c", align_bytes=64)
-        cs_pool = keep.tile([P, T // PACK], I32, name="cs_pool", tag="cs_then_q", align_bytes=64)
-        lse_rows = keep.tile([P, NQ], F32, name="lse_rows", align_bytes=64)
+        q_raw = keep.tile([P, PACK, NQ], F32, name="q_raw", align_bytes=256)
+        k_pool = keep.tile([P, T], I32, name="k_pool", align_bytes=256)
+        c_head = keep.tile([P, C_HEAD], I32, name="c_head", align_bytes=256)
+        ks_pool = keep.tile([P, T // PACK], I32, name="ks_pool", tag="ks_then_c", align_bytes=256)
+        cs_pool = keep.tile([P, T // PACK], I32, name="cs_pool", tag="cs_then_q", align_bytes=256)
+        lse_rows = keep.tile([P, NQ], F32, name="lse_rows", align_bytes=256)
         ident = keep.tile([P, P], F32, name="ident", align_bytes=64)
-        k_plane = keep.tile([P, N // PACK], I32, name="k_plane", align_bytes=64)
-        c_plane = keep.tile([P, N // PACK], I32, name="c_plane", align_bytes=64)
+        k_plane = keep.tile([P, N // PACK], I32, name="k_plane", align_bytes=256)
+        c_plane = keep.tile([P, N // PACK], I32, name="c_plane", align_bytes=256)
 
         nc.vector.memset(cs_pool[:], 0)
         nc.vector.memset(ks_pool[0:K_FIRST, :], 0)
@@ -79,12 +79,12 @@ def tile_attend_dupkl_topk_kernel(tc, qT, k_words, k_scales, c_words, c_scales, 
                 source = rows[first + j * step : first + ROWS * step : PACK * step, :].bitcast(I32)
                 nc.sync.dma_start(plane[start + j : P : QUADRANT, :], source)
 
-        ks_rows = keep.tile([P, N], U8, name="ks_rows", align_bytes=64)
+        ks_rows = keep.tile([P, N], U8, name="ks_rows", align_bytes=256)
         nc.vector.tensor_copy(ks_rows[:], ks_pool[:].bitcast(U8).indirect(offsets[:]))
         move_rows(k_plane, 0, ks_rows, K_FIRST, 1, range(PACK))
-        c_pool = keep.tile([P, T], I32, name="c_pool", tag="ks_then_c", align_bytes=64)
+        c_pool = keep.tile([P, T], I32, name="c_pool", tag="ks_then_c", align_bytes=256)
         nc.sync.dma_start(c_pool[:, C_HEAD:T], c_rows[:, C_HEAD:T])
-        cs_rows = keep.tile([P, N], U8, name="cs_rows", align_bytes=64)
+        cs_rows = keep.tile([P, N], U8, name="cs_rows", align_bytes=256)
         nc.vector.tensor_copy(cs_rows[:], cs_pool[:].bitcast(U8).indirect(offsets[:]))
 
         q_bf = keep.tile([P, QT, P, PACK], BF16, name="q_bf", align_bytes=64)
@@ -93,7 +93,7 @@ def tile_attend_dupkl_topk_kernel(tc, qT, k_words, k_scales, c_words, c_scales, 
         move_rows(c_plane, C_PLANE, cs_rows, C_FIRST, C_STEP, range(PACK))
         k_bytes = k_plane[:].bitcast(U8)
         c_bytes = c_plane[C_PLANE:P, :].bitcast(U8)
-        q_codes = keep.tile([P, NQ], U32, name="q_codes", tag="cs_then_q", align_bytes=64)
+        q_codes = keep.tile([P, NQ], U32, name="q_codes", tag="cs_then_q", align_bytes=256)
         q_scales = keep.tile([P, NQ], U8, name="q_scales", align_bytes=64)
         nc.vector.quantize_mx(
             out=q_codes[:].bitcast(FP8X4),
@@ -184,7 +184,7 @@ def tile_attend_dupkl_topk_kernel(tc, qT, k_words, k_scales, c_words, c_scales, 
 
         out_tiles = out[0].rearrange("(t p) n -> p t n", t=QT)
         diff = keep.tile([P, QT, N], F32, name="diff", align_bytes=64)
-        res = keep.tile([P, QT, N], F32, name="res", align_bytes=64)
+        res = keep.tile([P, QT, N], F32, name="res", align_bytes=256)
 
         def subtract(t, b):
             cols = slice(b * PIECE, (b + 1) * PIECE)

@@ -24,7 +24,7 @@ PER_COLUMN = 16
 ROWS = 16
 QUADRANT = 32
 K_FIRST = 2 * QUADRANT - ROWS
-C_FIRST = 2 * QUADRANT
+C_FIRST = QUADRANT
 C_STEP = PACK
 C_PLANE = 4
 LSE_ROW = P - 2
@@ -63,7 +63,7 @@ def tile_attend_dupkl_topk_kernel(tc, qT, k_words, k_scales, c_words, c_scales, 
         nc.sync.dma_start(q_raw[:], qT[0].rearrange("(p j) w -> p j w", j=PACK))
         nc.scalar.dma_start(lse_rows[LSE_ROW : LSE_ROW + 1, :], ls[0].rearrange("q o -> o q"))
         nc.scalar.dma_start(lse_rows[LSE_ROW + 1 : P, :], l2[0].rearrange("q o -> o q"))
-        nc.sync.dma_start(cs_pool[C_FIRST:P:C_STEP, :], c_scales[0].bitcast(I32))
+        nc.sync.dma_start(cs_pool[C_FIRST : C_FIRST + ROWS * C_STEP : C_STEP, :], c_scales[0].bitcast(I32))
         nc.sync.dma_start(k_pool[:], k_words[0].rearrange("p n t -> p (n t)").bitcast(I32))
         c_rows = c_words[0].rearrange("p n t -> p (n t)").bitcast(I32)
         nc.sync.dma_start(c_head[:], c_rows[:, 0:C_HEAD])

@@ -28,7 +28,7 @@ C_FIRST = QUADRANT
 C_STEP = PACK
 C_PLANE = 4
 LSE_ROW = P - 2
-C_HEAD = 512
+C_HEAD = 640
 LAST = 64
 PIECE = 128
 

from contextlib import ExitStack

import concourse.mybir as mybir
from concourse.masks import make_identity

N, T, D, NQ = 512, 2048, 512, 256
FLOPS = 2 * 2 * NQ * D * N

F32 = mybir.dt.float32
BF16 = mybir.dt.bfloat16
I32 = mybir.dt.int32
U32 = mybir.dt.uint32
U16 = mybir.dt.uint16
U8 = mybir.dt.uint8
FP8X4 = mybir.dt.float8_e4m3fn_x4
ACT = mybir.ActivationFunctionType
ALU = mybir.AluOpType

P = 128
PACK = 4
QT = NQ // P
HALF = N // 2
PER_COLUMN = 16
ROWS = 16
QUADRANT = 32
K_FIRST = 2 * QUADRANT - ROWS
C_FIRST = QUADRANT
C_STEP = PACK
C_PLANE = 4
LSE_ROW = P - 2
C_HEAD = 640
LAST = 64
PIECE = 128


def tile_attend_dupkl_topk_kernel(tc, qT, k_words, k_scales, c_words, c_scales, ls, l2, offs, out):
    nc = tc.nc
    with ExitStack() as ctx:
        keep = ctx.enter_context(tc.tile_pool(name="keep", bufs=1))
        psum = ctx.enter_context(tc.psum_pool(name="psum", bufs=1))

        offsets = keep.tile([P, N // PER_COLUMN], U16, name="offsets")
        q_raw = keep.tile([P, PACK, NQ], F32, name="q_raw", align_bytes=256)
        k_pool = keep.tile([P, T], I32, name="k_pool", align_bytes=256)
        c_head = keep.tile([P, C_HEAD], I32, name="c_head", align_bytes=256)
        ks_pool = keep.tile([P, T // PACK], I32, name="ks_pool", tag="ks_then_c", align_bytes=256)
        cs_pool = keep.tile([P, T // PACK], I32, name="cs_pool", tag="cs_then_q", align_bytes=256)
        lse_rows = keep.tile([P, NQ], F32, name="lse_rows", align_bytes=256)
        ident = keep.tile([P, P], F32, name="ident", align_bytes=64)
        k_plane = keep.tile([P, N // PACK], I32, name="k_plane", align_bytes=256)
        c_plane = keep.tile([P, N // PACK], I32, name="c_plane", align_bytes=256)

        nc.vector.memset(cs_pool[:], 0)
        nc.vector.memset(ks_pool[0:K_FIRST, :], 0)
        nc.vector.memset(ks_pool[K_FIRST + ROWS : P, :], 0)
        nc.vector.memset(k_plane[:], 0)
        nc.vector.memset(c_plane[:], 0)
        nc.gpsimd.memset(lse_rows[0:LSE_ROW, :], 0.0)
        make_identity(nc, ident[:])

        nc.sync.dma_start(offsets[:], offs)
        nc.scalar.dma_start(ks_pool[K_FIRST : K_FIRST + ROWS, :], k_scales[0].bitcast(I32))
        nc.sync.dma_start(q_raw[:], qT[0].rearrange("(p j) w -> p j w", j=PACK))
        nc.scalar.dma_start(lse_rows[LSE_ROW : LSE_ROW + 1, :], ls[0].rearrange("q o -> o q"))
        nc.scalar.dma_start(lse_rows[LSE_ROW + 1 : P, :], l2[0].rearrange("q o -> o q"))
        nc.sync.dma_start(cs_pool[C_FIRST : C_FIRST + ROWS * C_STEP : C_STEP, :], c_scales[0].bitcast(I32))
        nc.sync.dma_start(k_pool[:], k_words[0].rearrange("p n t -> p (n t)").bitcast(I32))
        c_rows = c_words[0].rearrange("p n t -> p (n t)").bitcast(I32)
        nc.sync.dma_start(c_head[:], c_rows[:, 0:C_HEAD])

        lse_cols = psum.tile([P, QT, P], F32, name="lse_cols", tag="lse_then_z")
        for t in range(QT):
            nc.tensor.transpose(lse_cols[:, t, :], lse_rows[:, t * P : (t + 1) * P], ident[:])
        neg = keep.tile([P, QT, 2], F32, name="neg", align_bytes=64)
        nc.scalar.mul(neg[:], lse_cols[:, :, LSE_ROW:P], -1.0)

        def move_rows(plane, start, rows, first, step, places):
            for j in places:
                source = rows[first + j * step : first + ROWS * step : PACK * step, :].bitcast(I32)
                nc.sync.dma_start(plane[start + j : P : QUADRANT, :], source)

        ks_rows = keep.tile([P, N], U8, name="ks_rows", align_bytes=256)
        nc.vector.tensor_copy(ks_rows[:], ks_pool[:].bitcast(U8).indirect(offsets[:]))
        move_rows(k_plane, 0, ks_rows, K_FIRST, 1, range(PACK))
        c_pool = keep.tile([P, T], I32, name="c_pool", tag="ks_then_c", align_bytes=256)
        nc.sync.dma_start(c_pool[:, C_HEAD:T], c_rows[:, C_HEAD:T])
        cs_rows = keep.tile([P, N], U8, name="cs_rows", align_bytes=256)
        nc.vector.tensor_copy(cs_rows[:], cs_pool[:].bitcast(U8).indirect(offsets[:]))

        q_bf = keep.tile([P, QT, P, PACK], BF16, name="q_bf", align_bytes=64)
        nc.scalar.copy(q_bf[:], q_raw[:].rearrange("p j (t m) -> p t m j", t=QT))

        move_rows(c_plane, C_PLANE, cs_rows, C_FIRST, C_STEP, range(PACK))
        k_bytes = k_plane[:].bitcast(U8)
        c_bytes = c_plane[C_PLANE:P, :].bitcast(U8)
        q_codes = keep.tile([P, NQ], U32, name="q_codes", tag="cs_then_q", align_bytes=256)
        q_scales = keep.tile([P, NQ], U8, name="q_scales", align_bytes=64)
        nc.vector.quantize_mx(
            out=q_codes[:].bitcast(FP8X4),
            scales=q_scales[:],
            in_=q_bf[:].rearrange("p t m j -> p (t m j)"),
        )

        minus_bf = keep.tile([P, P * PACK], BF16, name="minus_bf", align_bytes=64)
        nc.scalar.mul(minus_bf[:], q_bf[:, QT - 1].rearrange("p m j -> p (m j)"), -1.0)
        minus_codes = keep.tile([P, P], U32, name="minus_codes", align_bytes=64)
        minus_scales = keep.tile([P, P], U8, name="minus_scales", align_bytes=64)
        nc.vector.quantize_mx(out=minus_codes[:].bitcast(FP8X4), scales=minus_scales[:], in_=minus_bf[:])
        lse_gap = keep.tile([P, 1], F32, name="lse_gap", align_bytes=64)
        nc.vector.tensor_sub(lse_gap[:], neg[:, QT - 1, 0:1], neg[:, QT - 1, 1:2])

        def gather_words(pool, name, width):
            runs = []
            for n0 in range(0, N, width):
                words = keep.tile([P, width], U32, name=f"{name}{n0}", align_bytes=64)
                entries = offsets[:, n0 // PER_COLUMN : (n0 + width) // PER_COLUMN]
                nc.vector.tensor_copy(words[:], pool[:].bitcast(U32).indirect(entries))
                runs.append(words)
            return runs

        def product(scores, codes, scales, words, scale_bytes, start=True, stop=True):
            nc.tensor.matmul_mx(
                out=scores,
                lhsT=codes.bitcast(FP8X4),
                lhsT_scale=scales,
                rhs=words.bitcast(FP8X4),
                rhs_scale=scale_bytes,
                start=start,
                stop=stop,
            )

        def queries(t):
            return q_codes[:, t * P : (t + 1) * P], q_scales[:, t * P : (t + 1) * P]

        kw = gather_words(k_pool, "kw", HALF)
        nc.vector.tensor_copy(c_pool[:, 0:C_HEAD], c_head[:])
        ea = keep.tile([P, QT, N], F32, name="ea", align_bytes=64)
        for h in range(2):
            for t in reversed(range(QT)):
                a = psum.tile([P, HALF], F32, name=f"a{h}{t}", tag=f"scores{t}_{h}")
                product(a[:], *queries(t), kw[h][:], k_bytes[:, h * HALF : (h + 1) * HALF])
                nc.scalar.activation(ea[:, t, h * HALF : (h + 1) * HALF], a[:], ACT.Exp, bias=neg[:, t, 0:1])

        last = QT - 1
        gap = {}
        for b, tag in ((2, "lse_then_z"), (3, "scores1_0")):
            gap[b] = psum.tile([P, PIECE], F32, name=f"gap{b}", tag=tag)
            at = b * PIECE - HALF
            product(gap[b][:], *queries(last), kw[1][:, at : at + PIECE], k_bytes[:, b * PIECE : (b + 1) * PIECE], stop=False)
        minus_ea = keep.tile([P, HALF], F32, name="minus_ea", align_bytes=64)
        nc.scalar.mul(minus_ea[:], ea[:, last, HALF:N], -1.0)

        cw = gather_words(c_pool, "cw", PIECE)
        ez = keep.tile([P, QT, N], F32, name="ez", align_bytes=64)
        lead = keep.tile([P, HALF], F32, name="lead", align_bytes=64)
        ratio = keep.tile([P, HALF], F32, name="ratio", align_bytes=64)
        banks = ["z0", "z1", "z2", "scores0_1", "scores0_0", "scores1_1"]

        def exp_draft(t, b):
            cols = slice(b * PIECE, (b + 1) * PIECE)
            z = psum.tile([P, PIECE], F32, name=f"z{t}_{b}", tag=banks.pop(0))
            product(z[:], *queries(t), cw[b][:], c_bytes[:, cols])
            nc.scalar.activation(ez[:, t, cols], z[:], ACT.Exp, bias=neg[:, t, 1:2])

        def relu_gap(b):
            product(gap[b][:], minus_codes[:], minus_scales[:], cw[b][:], c_bytes[:, b * PIECE : (b + 1) * PIECE], start=False)
            at = b * PIECE - HALF
            nc.scalar.activation(lead[:, at : at + PIECE], gap[b][:], ACT.Relu, bias=lse_gap[:])

        def exp_gap(lo, hi):
            nc.scalar.activation(ratio[:, lo:hi], lead[:, lo:hi], ACT.Exp, scale=-1.0)

        for b in range(2):
            for t in range(QT):
                exp_draft(t, b)
        exp_draft(0, 2)
        relu_gap(2)
        exp_draft(0, 3)
        relu_gap(3)
        wide = HALF - LAST
        exp_gap(0, PIECE)
        exp_gap(PIECE, wide)
        exp_gap(wide, HALF)

        out_tiles = out[0].rearrange("(t p) n -> p t n", t=QT)
        diff = keep.tile([P, QT, N], F32, name="diff", align_bytes=64)
        res = keep.tile([P, QT, N], F32, name="res", align_bytes=256)

        def subtract(t, b):
            cols = slice(b * PIECE, (b + 1) * PIECE)
            nc.vector.tensor_sub(diff[:, t, cols], ea[:, t, cols], ez[:, t, cols])

        def clamp(t, lo, hi):
            nc.vector.tensor_scalar_max(res[:, t, lo:hi], diff[:, t, lo:hi], 0.0)

        def finish(lo, hi):
            nc.vector.scalar_tensor_tensor(
                res[:, last, HALF + lo : HALF + hi], ratio[:, lo:hi], 1.0, minus_ea[:, lo:hi], ALU.subtract, ALU.mult
            )

        def store(t, lo, hi):
            nc.sync.dma_start(out_tiles[:, t, lo:hi], res[:, t, lo:hi])

        subtract(0, 0)
        subtract(1, 0)
        subtract(0, 1)
        clamp(0, 0, PIECE)
        subtract(1, 1)
        clamp(0, PIECE, HALF)
        store(0, 0, HALF)
        subtract(0, 2)
        clamp(1, 0, HALF)
        store(1, 0, HALF)
        subtract(0, 3)
        finish(0, PIECE)
        clamp(0, HALF, N)
        store(0, HALF, N)
        finish(PIECE, wide)
        finish(wide, HALF)
        store(1, HALF, N)
